import numpy as np
import ml_dtypes


def mxq(x, axis, fmt="e4m3"):
    dtype, down = {"e4m3": (ml_dtypes.float8_e4m3fn, 7), "e5m2": (ml_dtypes.float8_e5m2, 14)}[fmt]
    v = np.moveaxis(np.asarray(x, np.float32).astype(ml_dtypes.bfloat16).astype(np.float64), axis, -1)
    blocks = v.reshape(v.shape[:-1] + (-1, 32))
    amax = np.abs(blocks).max(-1, keepdims=True)
    byte = np.maximum(np.where(amax > 0, np.frexp(amax)[1] - 1 + 127, 0) - down, 1)
    scale = np.exp2(byte - 127.0)
    codes = (blocks / scale).astype(np.float32).astype(dtype).astype(np.float64)
    return np.moveaxis((codes * scale).reshape(v.shape), -1, axis)


WIDE = False


def mx_kscale(k):
    if not WIDE:
        return np.ones(k)
    levels = np.array([10, -10, 5, -5, 0])
    if k % 512:
        return np.exp2(np.random.permutation(np.resize(levels, k // 32))).repeat(32)
    a = np.empty((k // 512, 16))
    for p in range(k // 512):
        a[p, :8] = np.random.permutation(np.resize(levels, 8))
        for g in range(8):
            far = levels[np.abs(levels - a[p, g]) >= 10]
            a[p, g + 8] = far[np.random.randint(len(far))]
    return np.exp2(a.ravel()).repeat(32)


def f64(x):
    return np.asarray(x).astype(np.float64)


def striped(idx):
    return np.tile(idx.reshape(-1, 16).T, (8, 1)).astype(np.uint16)


def unstriped(offs):
    return offs[:16].T.reshape(-1).astype(np.int64)


E2M1 = np.array([0.0, 0.5, 1.0, 1.5, 2.0, 3.0, 4.0, 6.0, -0.0, -0.5, -1.0, -1.5, -2.0, -3.0, -4.0, -6.0])


def pack_weight(w, fmt):
    k, n = w.shape
    w = f64(np.asarray(w, np.float32).astype(ml_dtypes.bfloat16)).reshape(k // 32, 32, n)
    amax = np.abs(w).max(1)
    if fmt == "e4m3":
        byte = np.frexp(amax)[1] - 1 + 127 - 7
    else:
        mant, ex = np.frexp(amax / 6.0)
        byte = np.where(mant > 0.5, ex, ex - 1) + 127
    byte = np.clip(np.where(amax > 0, byte, 1), 1, 254)
    scaled = (w * np.exp2(127.0 - byte)[:, None, :]).reshape(k, n).astype(np.float32)
    by_word = np.ascontiguousarray(scaled.reshape(k // 512, 128, 4, n).transpose(0, 1, 3, 2))
    if fmt == "e4m3":
        words = by_word.astype(ml_dtypes.float8_e4m3fn).view(np.uint8)
    else:
        c = by_word.astype(ml_dtypes.float4_e2m1fn).view(np.uint8) & 0xF
        words = (c[..., 0::2] | (c[..., 1::2] << 4)).reshape(k // 512, 128, 2 * n)
    return np.ascontiguousarray(words), np.ascontiguousarray(byte.astype(np.uint8).reshape(k // 512, 16, n))


def unpack_weight(words, scales, fmt):
    g, _, n = scales.shape
    words = np.ascontiguousarray(words).reshape(g, 128, n, -1)
    if fmt == "e4m3":
        vals = words.view(ml_dtypes.float8_e4m3fn).astype(np.float64)
    else:
        nib = np.empty((g, 128, n, 4), np.uint8)
        nib[..., 0::2] = words & 0xF
        nib[..., 1::2] = words >> 4
        vals = E2M1[nib]
    vals = vals * np.repeat(np.exp2(scales.astype(np.float64) - 127.0), 8, axis=1)[..., None]
    return vals.transpose(0, 1, 3, 2).reshape(g * 512, n)


def pack_table(v):
    words, scales = pack_weight(v, "e4m3")
    return np.concatenate([words.reshape(words.shape[0], -1), scales.reshape(scales.shape[0], -1)], axis=1)


def unpack_table(tab):
    g, t = tab.shape[0], tab.shape[1] // 528
    return unpack_weight(tab[:, :512 * t].reshape(g, 128, t, 4), tab[:, 512 * t:].reshape(g, 16, t), "e4m3")


K, H, M, T, S = 512, 1024, 256, 4096, 1536


def setup_inputs():
    n = np.random.standard_normal
    s = mx_kscale(K)[:, None]
    u = mx_kscale(H)[:, None]
    w2 = 1.4 * n((H, M)) / np.sqrt(H) / u
    p_w8 = pack_weight(w2[:512], "e4m3")
    p_w4 = pack_weight(w2[512:], "e2m1")
    return {
        "tab": pack_table(n((K, T)) * s),
        "w1": (n((K, H)) / np.sqrt(K) / s * u.T).astype(np.float32),
        "w8_words": p_w8[0],
        "w8_scales": p_w8[1],
        "w4_words": p_w4[0],
        "w4_scales": p_w4[1],
        "b": (0.3 * n(256)).astype(np.float32),
        "offs": striped(np.random.permutation(T)[:S]),
    }


def reference(tab, w1, w8_words, w8_scales, w4_words, w4_scales, b, offs):
    tab_ = unpack_table(tab)[:, unstriped(offs)]
    w1_ = mxq(f64(w1), 0, "e4m3")
    w8_ = unpack_weight(w8_words, w8_scales, "e4m3")
    w4_ = unpack_weight(w4_words, w4_scales, "e2m1")
    h_ = mxq(np.maximum(w1_.T @ tab_, 0.0), 0, "e4m3")
    y = w8_.T @ h_[:512] + w4_.T @ h_[512:]
    return y + f64(b)[:, None]

@@ -1,0 +1,231 @@
+from contextlib import ExitStack
+
+import concourse.mybir as mybir
+
+K, H, M, T, S = 512, 1024, 256, 4096, 1536
+FLOPS = 2 * S * (K * H + H * M)
+
+F32 = mybir.dt.float32
+BF16 = mybir.dt.bfloat16
+I32 = mybir.dt.int32
+U32 = mybir.dt.uint32
+U16 = mybir.dt.uint16
+U8 = mybir.dt.uint8
+FP8X4 = mybir.dt.float8_e4m3fn_x4
+FP4X4 = mybir.dt.float4_e2m1fn_x4
+RELU = mybir.ActivationFunctionType.Relu
+IDENTITY = mybir.ActivationFunctionType.Identity
+ADD = mybir.AluOpType.add
+MULT = mybir.AluOpType.mult
+
+P = 128
+CHUNK = 512
+BLOCK = 128
+GROUP = 512
+CHUNKS = S // CHUNK
+BLOCKS = CHUNK // BLOCK
+GROUPS = H // GROUP
+PIECE = 256
+
+CONVERT = ["s","s","v","v"]
+RELU_ENGINE = [["ssss","sssv"],["ssss","svsv"],["svsv","svsv"]]
+GROUPED_TAG = ["turn","turn"]
+OUT_ENGINE = ["ss","sv","sv"]
+
+
+def tile_list_tabmlp_mix_bias_kernel(
+    tc, tab, w1, w8_words, w8_scales, w4_words, w4_scales, b, offs, out
+):
+    nc = tc.nc
+    with ExitStack() as ctx:
+        keep = ctx.enter_context(tc.tile_pool(name="keep", bufs=1))
+        hidden_psum = ctx.enter_context(tc.psum_pool(name="hidden_psum", bufs=6))
+        out_psum = ctx.enter_context(tc.psum_pool(name="out_psum", bufs=2))
+
+        offsets = keep.tile([P, S // 16], U16, name="offsets")
+        nc.sync.dma_start(offsets[:], offs)
+
+        table_words = keep.tile([P, T], I32, name="table_words", align_bytes=64)
+        words_hbm = tab[0, 0 : 512 * T].rearrange("(p c) -> p c", p=P).bitcast(I32)
+        for half in range(2):
+            cols = slice(half * T // 2, (half + 1) * T // 2)
+            nc.sync.dma_start(table_words[:, cols], words_hbm[:, cols])
+
+
+        table_scales = keep.tile([P, T], U8, name="table_scales", align_bytes=64)
+        nc.vector.memset(table_scales[:].bitcast(I32), 0)
+        w1_hbm = w1.rearrange("(p j) c -> p j c", j=4)
+        w1_raw = []
+
+        def load_w1(g):
+            for piece in range(g * GROUP // PIECE, (g + 1) * GROUP // PIECE):
+                raw = keep.tile([P, 4, PIECE], F32, name=f"w1_raw{piece}")
+                nc.sync.dma_start(raw[:], w1_hbm[:, :, piece * PIECE : (piece + 1) * PIECE])
+                w1_raw.append(raw)
+
+        load_w1(0)
+        scales_hbm = tab[0, 512 * T : 528 * T].rearrange("(q r t) -> r q t", q=4, r=4).bitcast(I32)
+        for r in range(4):
+            nc.sync.dma_start(table_scales[r:P:32, :].bitcast(I32), scales_hbm[r])
+        load_w1(1)
+
+        w8 = keep.tile([P, M], I32, name="w8", align_bytes=64)
+        nc.sync.dma_start(w8[:], w8_words[0].rearrange("p n i -> p (n i)").bitcast(I32))
+        w4 = keep.tile([P, 2 * M], U8, name="w4", align_bytes=64)
+        nc.sync.dma_start(w4[:].bitcast(I32), w4_words[0].bitcast(I32))
+
+        w_scales = keep.tile([P, 2, M], U8, name="w_scales", align_bytes=64)
+        nc.vector.memset(w_scales[:].rearrange("p g n -> p (g n)").bitcast(I32), 0)
+        for g, src in enumerate((w8_scales, w4_scales)):
+            rows = src[0].rearrange("(q r) n -> r q n", r=4).bitcast(I32)
+            for r in range(4):
+                nc.sync.dma_start(w_scales[r:P:32, g, :].bitcast(I32), rows[r])
+        bias = keep.tile([P, 2], F32, name="bias")
+        nc.sync.dma_start(bias[:], b.rearrange("(m p) -> p m", p=P))
+
+        x_words = []
+        x_scales = []
+
+        def listed(c):
+            return offsets[:, c * (CHUNK // 16) : (c + 1) * (CHUNK // 16)]
+
+        def gather_words(c):
+            words = keep.tile([P, CHUNK], U32, name=f"x_words{c}", align_bytes=64)
+            nc.vector.tensor_copy(words[:], table_words[:].bitcast(U32).indirect(listed(c)))
+            x_words.append(words)
+
+        def gather_scales(first, count, tag):
+            scales = keep.tile([P, count, CHUNK], U8, name=f"x_scales{first}", tag=tag, align_bytes=64)
+            for i in range(count):
+                nc.vector.tensor_copy(scales[:, i, :], table_scales[:].indirect(listed(first + i)))
+                x_scales.append(scales[:, i, :])
+
+        w1_codes = []
+        w1_scales = []
+
+        def prepare_w1(g):
+            grouped = keep.tile([P, 4 * GROUP], BF16, name=f"w1_grouped{g}", tag=GROUPED_TAG[g], align_bytes=64)
+            order = grouped[:].rearrange("p (t m j) -> p m j t", t=4, j=4)
+            per_group = GROUP // PIECE
+            for i in range(per_group):
+                piece = g * per_group + i
+                m = slice(i * PIECE // 4, (i + 1) * PIECE // 4)
+                dst = order[:, m, :, :]
+                src = w1_raw[piece][:].rearrange("p j (m t) -> p m j t", t=4)
+                engine = CONVERT[piece]
+                if engine == "s":
+                    nc.scalar.copy(dst, src)
+                elif engine == "g":
+                    nc.gpsimd.tensor_scalar(dst, src, 1.0, 0.0, MULT, ADD)
+                else:
+                    nc.vector.tensor_copy(dst, src)
+            codes = keep.tile([P, GROUP], U32, name=f"w1_codes{g}", align_bytes=64)
+            scales = keep.tile([P, GROUP], U8, name=f"w1_scales{g}", align_bytes=64)
+            nc.vector.quantize_mx(out=codes[:].bitcast(FP8X4), scales=scales[:], in_=grouped[:])
+            w1_codes.append(codes)
+            w1_scales.append(scales)
+
+        h_grouped = {}
+        h_codes = {}
+        h_scales = {}
+        for c in range(CHUNKS):
+            for g in range(GROUPS):
+                h_grouped[c, g] = keep.tile([P, 4 * CHUNK], BF16, name=f"h_grouped{c}{g}", align_bytes=64)
+                h_codes[c, g] = keep.tile([P, CHUNK], U32, name=f"h_codes{c}{g}", align_bytes=64)
+                h_scales[c, g] = keep.tile([P, CHUNK], U8, name=f"h_scales{c}{g}", align_bytes=64)
+
+        def hidden(c, g, block):
+            bank = hidden_psum.tile([P, 4, BLOCK], F32, name="bank")
+            cols = slice(block * BLOCK, (block + 1) * BLOCK)
+            for t in range(4):
+                rows = slice(t * P, (t + 1) * P)
+                nc.tensor.matmul_mx(
+                    out=bank[:, t, :],
+                    lhsT=w1_codes[g][:, rows].bitcast(FP8X4),
+                    lhsT_scale=w1_scales[g][:, rows],
+                    rhs=x_words[c][:, cols].bitcast(FP8X4),
+                    rhs_scale=x_scales[c][:, cols],
+                    start=True,
+                    stop=True,
+                )
+            dst = h_grouped[c, g][:, 4 * BLOCK * block : 4 * BLOCK * (block + 1)].rearrange("p (n t) -> p n t", t=4)
+            src = bank[:].rearrange("p t n -> p n t")
+            if RELU_ENGINE[c][g][block] == "s":
+                nc.scalar.activation(dst, src, RELU)
+            else:
+                nc.vector.tensor_scalar_max(dst, src, 0.0)
+
+        def quantize(c, g, block0, blocks):
+            cols = slice(block0 * BLOCK, (block0 + blocks) * BLOCK)
+            nc.vector.quantize_mx(
+                out=h_codes[c, g][:, cols].bitcast(FP8X4),
+                scales=h_scales[c, g][:, cols],
+                in_=h_grouped[c, g][:, 4 * BLOCK * block0 : 4 * BLOCK * (block0 + blocks)],
+            )
+
+        out_hbm = out.rearrange("(m p) j -> p m j", p=P)
+
+        def output(c, block0, blocks, width, engines):
+            total = blocks * BLOCK
+            stage = keep.tile([P, 2, total], F32, name=f"stage{c}_{block0}")
+            for m in range(2):
+                acc = out_psum.tile([P, CHUNK], F32, name="acc")
+                rows = slice(m * P, (m + 1) * P)
+                for n in range(0, total, width):
+                    cols = slice(block0 * BLOCK + n, block0 * BLOCK + n + width)
+                    nc.tensor.matmul_mx(
+                        out=acc[:, n : n + width],
+                        lhsT=w8[:, rows].bitcast(FP8X4),
+                        lhsT_scale=w_scales[:, 0, rows],
+                        rhs=h_codes[c, 0][:, cols].bitcast(FP8X4),
+                        rhs_scale=h_scales[c, 0][:, cols],
+                        start=True,
+                        stop=False,
+                    )
+                    nc.tensor.matmul_mx(
+                        out=acc[:, n : n + width],
+                        lhsT=w4[:, 2 * m * P : 2 * (m + 1) * P].bitcast(FP4X4),
+                        lhsT_scale=w_scales[:, 1, rows],
+                        rhs=h_codes[c, 1][:, cols].bitcast(FP8X4),
+                        rhs_scale=h_scales[c, 1][:, cols],
+                        start=False,
+                        stop=True,
+                    )
+                if engines[m] == "s":
+                    nc.scalar.activation(stage[:, m, :], acc[:, 0:total], IDENTITY, bias=bias[:, m : m + 1])
+                else:
+                    nc.vector.tensor_scalar(stage[:, m, :], acc[:, 0:total], bias[:, m : m + 1], None, ADD)
+            first = c * CHUNK + block0 * BLOCK
+            nc.sync.dma_start(out_hbm[:, :, first : first + total], stage[:])
+
+        for c in range(CHUNKS):
+            gather_words(c)
+        prepare_w1(0)
+        gather_scales(0, 1, "x_scales0")
+        for block in range(BLOCKS):
+            hidden(0, 0, block)
+        gather_scales(1, 2, "x_scales1")
+        for block in range(BLOCKS):
+            hidden(1, 0, block)
+        prepare_w1(1)
+        quantize(0, 0, 0, 4)
+        for block in range(BLOCKS):
+            hidden(0, 1, block)
+        quantize(1, 0, 0, 4)
+        quantize(0, 1, 0, 4)
+        for block in range(BLOCKS):
+            hidden(1, 1, block)
+        output(0, 0, 4, 512, OUT_ENGINE[0])
+        quantize(1, 1, 0, 4)
+        for block in range(BLOCKS):
+            hidden(2, 0, block)
+        output(1, 0, 4, 512, OUT_ENGINE[1])
+        quantize(2, 0, 0, 4)
+        for block in range(BLOCKS):
+            hidden(2, 1, block)
+            if block == 1:
+                quantize(2, 1, 0, 2)
+        output(2, 0, 2, 128, OUT_ENGINE[2])
+        quantize(2, 1, 2, 1)
+        quantize(2, 1, 3, 1)
+        output(2, 2, 2, 128, OUT_ENGINE[2])

@@ -27,10 +27,10 @@ BLOCKS = CHUNK // BLOCK
 GROUPS = H // GROUP
 PIECE = 256
 
-CONVERT = ["s","s","v","v"]
-RELU_ENGINE = [["ssss","sssv"],["ssss","svsv"],["svsv","svsv"]]
-GROUPED_TAG = ["turn","turn"]
-OUT_ENGINE = ["ss","sv","sv"]
+
+FIRST_COLUMNS = 1024
+SCALAR_SHARE = 24
+FIRST_VECTOR_BANK = 9
 
 
 def tile_list_tabmlp_mix_bias_kernel(
@@ -39,35 +39,27 @@ def tile_list_tabmlp_mix_bias_kernel(
     nc = tc.nc
     with ExitStack() as ctx:
         keep = ctx.enter_context(tc.tile_pool(name="keep", bufs=1))
-        hidden_psum = ctx.enter_context(tc.psum_pool(name="hidden_psum", bufs=6))
-        out_psum = ctx.enter_context(tc.psum_pool(name="out_psum", bufs=2))
+        psum = ctx.enter_context(tc.psum_pool(name="psum", bufs=8))
 
         offsets = keep.tile([P, S // 16], U16, name="offsets")
         nc.sync.dma_start(offsets[:], offs)
 
         table_words = keep.tile([P, T], I32, name="table_words", align_bytes=64)
-        words_hbm = tab[0, 0 : 512 * T].rearrange("(p c) -> p c", p=P).bitcast(I32)
-        for half in range(2):
-            cols = slice(half * T // 2, (half + 1) * T // 2)
-            nc.sync.dma_start(table_words[:, cols], words_hbm[:, cols])
-
-
         table_scales = keep.tile([P, T], U8, name="table_scales", align_bytes=64)
-        nc.vector.memset(table_scales[:].bitcast(I32), 0)
-        w1_hbm = w1.rearrange("(p j) c -> p j c", j=4)
-        w1_raw = []
-
-        def load_w1(g):
-            for piece in range(g * GROUP // PIECE, (g + 1) * GROUP // PIECE):
-                raw = keep.tile([P, 4, PIECE], F32, name=f"w1_raw{piece}")
-                nc.sync.dma_start(raw[:], w1_hbm[:, :, piece * PIECE : (piece + 1) * PIECE])
-                w1_raw.append(raw)
-
-        load_w1(0)
+        words_hbm = tab[0, 0 : 512 * T].rearrange("(p c) -> p c", p=P).bitcast(I32)
         scales_hbm = tab[0, 512 * T : 528 * T].rearrange("(q r t) -> r q t", q=4, r=4).bitcast(I32)
+        nc.vector.memset(table_scales[:].bitcast(I32), 0)
+        nc.sync.dma_start(table_words[:, 0:FIRST_COLUMNS], words_hbm[:, 0:FIRST_COLUMNS])
         for r in range(4):
             nc.sync.dma_start(table_scales[r:P:32, :].bitcast(I32), scales_hbm[r])
-        load_w1(1)
+        nc.sync.dma_start(table_words[:, FIRST_COLUMNS:T], words_hbm[:, FIRST_COLUMNS:T])
+
+        w1_hbm = w1.rearrange("(p j) c -> p j c", j=4)
+        w1_raw = []
+        for piece in range(H // PIECE):
+            raw = keep.tile([P, 4, PIECE], F32, name=f"w1_raw{piece}")
+            nc.sync.dma_start(raw[:], w1_hbm[:, :, piece * PIECE : (piece + 1) * PIECE])
+            w1_raw.append(raw)
 
         w8 = keep.tile([P, M], I32, name="w8", align_bytes=64)
         nc.sync.dma_start(w8[:], w8_words[0].rearrange("p n i -> p (n i)").bitcast(I32))
@@ -83,47 +75,37 @@ def tile_list_tabmlp_mix_bias_kernel(
         bias = keep.tile([P, 2], F32, name="bias")
         nc.sync.dma_start(bias[:], b.rearrange("(m p) -> p m", p=P))
 
-        x_words = []
-        x_scales = []
+        x_scales = keep.tile([P, S], U8, name="x_scales", align_bytes=64)
+        nc.vector.tensor_copy(x_scales[:], table_scales[:].indirect(offsets[:]))
 
-        def listed(c):
-            return offsets[:, c * (CHUNK // 16) : (c + 1) * (CHUNK // 16)]
+        x_words = {}
 
-        def gather_words(c):
-            words = keep.tile([P, CHUNK], U32, name=f"x_words{c}", align_bytes=64)
-            nc.vector.tensor_copy(words[:], table_words[:].bitcast(U32).indirect(listed(c)))
-            x_words.append(words)
+        def gather_words(c, tag):
+            words = keep.tile([P, CHUNK], U32, name=f"x_words{c}", tag=tag, align_bytes=64)
+            listed = offsets[:, c * (CHUNK // 16) : (c + 1) * (CHUNK // 16)]
+            nc.vector.tensor_copy(words[:], table_words[:].bitcast(U32).indirect(listed))
+            x_words[c] = words
 
-        def gather_scales(first, count, tag):
-            scales = keep.tile([P, count, CHUNK], U8, name=f"x_scales{first}", tag=tag, align_bytes=64)
-            for i in range(count):
-                nc.vector.tensor_copy(scales[:, i, :], table_scales[:].indirect(listed(first + i)))
-                x_scales.append(scales[:, i, :])
+        w1_grouped = {}
+        w1_codes = {}
+        w1_scales = {}
+        for g in range(GROUPS):
+            w1_grouped[g] = keep.tile([P, 4 * GROUP], BF16, name=f"w1_grouped{g}", tag=f"w1_grouped{g}", align_bytes=64)
+            w1_codes[g] = keep.tile([P, GROUP], U32, name=f"w1_codes{g}", align_bytes=64)
+            w1_scales[g] = keep.tile([P, GROUP], U8, name=f"w1_scales{g}", align_bytes=64)
 
-        w1_codes = []
-        w1_scales = []
+        def convert(piece, first, last, on_scalar):
+            g, i = divmod(piece, GROUP // PIECE)
+            order = w1_grouped[g][:].rearrange("p (t m j) -> p m j t", t=4, j=4)
+            dst = order[:, i * PIECE // 4 + first : i * PIECE // 4 + last, :, :]
+            src = w1_raw[piece][:].rearrange("p j (m t) -> p m j t", t=4)[:, first:last, :, :]
+            if on_scalar:
+                nc.scalar.copy(dst, src)
+            else:
+                nc.vector.tensor_copy(dst, src)
 
-        def prepare_w1(g):
-            grouped = keep.tile([P, 4 * GROUP], BF16, name=f"w1_grouped{g}", tag=GROUPED_TAG[g], align_bytes=64)
-            order = grouped[:].rearrange("p (t m j) -> p m j t", t=4, j=4)
-            per_group = GROUP // PIECE
-            for i in range(per_group):
-                piece = g * per_group + i
-                m = slice(i * PIECE // 4, (i + 1) * PIECE // 4)
-                dst = order[:, m, :, :]
-                src = w1_raw[piece][:].rearrange("p j (m t) -> p m j t", t=4)
-                engine = CONVERT[piece]
-                if engine == "s":
-                    nc.scalar.copy(dst, src)
-                elif engine == "g":
-                    nc.gpsimd.tensor_scalar(dst, src, 1.0, 0.0, MULT, ADD)
-                else:
-                    nc.vector.tensor_copy(dst, src)
-            codes = keep.tile([P, GROUP], U32, name=f"w1_codes{g}", align_bytes=64)
-            scales = keep.tile([P, GROUP], U8, name=f"w1_scales{g}", align_bytes=64)
-            nc.vector.quantize_mx(out=codes[:].bitcast(FP8X4), scales=scales[:], in_=grouped[:])
-            w1_codes.append(codes)
-            w1_scales.append(scales)
+        def quantize_w1(g):
+            nc.vector.quantize_mx(out=w1_codes[g][:].bitcast(FP8X4), scales=w1_scales[g][:], in_=w1_grouped[g][:])
 
         h_grouped = {}
         h_codes = {}
@@ -134,26 +116,35 @@ def tile_list_tabmlp_mix_bias_kernel(
                 h_codes[c, g] = keep.tile([P, CHUNK], U32, name=f"h_codes{c}{g}", align_bytes=64)
                 h_scales[c, g] = keep.tile([P, CHUNK], U8, name=f"h_scales{c}{g}", align_bytes=64)
 
+        banks_done = []
+
         def hidden(c, g, block):
-            bank = hidden_psum.tile([P, 4, BLOCK], F32, name="bank")
+            bank = psum.tile([P, 4 * BLOCK], F32, name="bank")
             cols = slice(block * BLOCK, (block + 1) * BLOCK)
+            listed = slice(c * CHUNK + block * BLOCK, c * CHUNK + (block + 1) * BLOCK)
             for t in range(4):
                 rows = slice(t * P, (t + 1) * P)
                 nc.tensor.matmul_mx(
-                    out=bank[:, t, :],
+                    out=bank[:, t * BLOCK : (t + 1) * BLOCK],
                     lhsT=w1_codes[g][:, rows].bitcast(FP8X4),
                     lhsT_scale=w1_scales[g][:, rows],
                     rhs=x_words[c][:, cols].bitcast(FP8X4),
-                    rhs_scale=x_scales[c][:, cols],
+                    rhs_scale=x_scales[:, listed],
                     start=True,
                     stop=True,
                 )
             dst = h_grouped[c, g][:, 4 * BLOCK * block : 4 * BLOCK * (block + 1)].rearrange("p (n t) -> p n t", t=4)
-            src = bank[:].rearrange("p t n -> p n t")
-            if RELU_ENGINE[c][g][block] == "s":
-                nc.scalar.activation(dst, src, RELU)
-            else:
+            src = bank[:].rearrange("p (t n) -> p n t", t=4)
+            number = len(banks_done)
+            banks_done.append(number)
+            if number >= FIRST_VECTOR_BANK and number % 2 == 1:
                 nc.vector.tensor_scalar_max(dst, src, 0.0)
+            else:
+                nc.scalar.activation(dst, src, RELU)
+
+        def hidden_chunk(c, g):
+            for block in range(BLOCKS):
+                hidden(c, g, block)
 
         def quantize(c, g, block0, blocks):
             cols = slice(block0 * BLOCK, (block0 + blocks) * BLOCK)
@@ -169,7 +160,7 @@ def tile_list_tabmlp_mix_bias_kernel(
             total = blocks * BLOCK
             stage = keep.tile([P, 2, total], F32, name=f"stage{c}_{block0}")
             for m in range(2):
-                acc = out_psum.tile([P, CHUNK], F32, name="acc")
+                acc = psum.tile([P, 4 * BLOCK], F32, name="bank")
                 rows = slice(m * P, (m + 1) * P)
                 for n in range(0, total, width):
                     cols = slice(block0 * BLOCK + n, block0 * BLOCK + n + width)
@@ -198,34 +189,36 @@ def tile_list_tabmlp_mix_bias_kernel(
             first = c * CHUNK + block0 * BLOCK
             nc.sync.dma_start(out_hbm[:, :, first : first + total], stage[:])
 
-        for c in range(CHUNKS):
-            gather_words(c)
-        prepare_w1(0)
-        gather_scales(0, 1, "x_scales0")
-        for block in range(BLOCKS):
-            hidden(0, 0, block)
-        gather_scales(1, 2, "x_scales1")
-        for block in range(BLOCKS):
-            hidden(1, 0, block)
-        prepare_w1(1)
+        gather_words(0, "x_words0")
+        gather_words(1, "x_words1")
+        convert(0, 0, PIECE // 4, True)
+        convert(1, 0, SCALAR_SHARE, True)
+        convert(1, SCALAR_SHARE, PIECE // 4, False)
+        quantize_w1(0)
+        gather_words(2, "w1_grouped0")
+        convert(2, 0, PIECE // 4, True)
+        hidden_chunk(0, 0)
+        convert(3, 0, PIECE // 4, False)
+        quantize_w1(1)
+        hidden_chunk(1, 0)
         quantize(0, 0, 0, 4)
-        for block in range(BLOCKS):
-            hidden(0, 1, block)
+        hidden_chunk(2, 0)
         quantize(1, 0, 0, 4)
-        quantize(0, 1, 0, 4)
-        for block in range(BLOCKS):
-            hidden(1, 1, block)
-        output(0, 0, 4, 512, OUT_ENGINE[0])
-        quantize(1, 1, 0, 4)
-        for block in range(BLOCKS):
-            hidden(2, 0, block)
-        output(1, 0, 4, 512, OUT_ENGINE[1])
+        hidden_chunk(0, 1)
         quantize(2, 0, 0, 4)
-        for block in range(BLOCKS):
-            hidden(2, 1, block)
-            if block == 1:
-                quantize(2, 1, 0, 2)
-        output(2, 0, 2, 128, OUT_ENGINE[2])
-        quantize(2, 1, 2, 1)
-        quantize(2, 1, 3, 1)
-        output(2, 2, 2, 128, OUT_ENGINE[2])
+        hidden(1, 1, 0)
+        hidden(1, 1, 1)
+        quantize(0, 1, 0, 4)
+        hidden(1, 1, 2)
+        hidden(1, 1, 3)
+        output(0, 0, 4, 512, "ss")
+        hidden(2, 1, 0)
+        hidden(2, 1, 1)
+        quantize(1, 1, 0, 4)
+        hidden(2, 1, 2)
+        hidden(2, 1, 3)
+        output(1, 0, 4, 512, "ss")
+        quantize(2, 1, 0, 2)
+        output(2, 0, 2, 128, "sv")
+        quantize(2, 1, 2, 2)
+        output(2, 2, 2, 128, "sv")

@@ -30,7 +30,6 @@ PIECE = 256
 
 FIRST_COLUMNS = 1024
 SCALAR_SHARE = 24
-FIRST_VECTOR_BANK = 9
 
 
 def tile_list_tabmlp_mix_bias_kernel(
@@ -137,7 +136,7 @@ def tile_list_tabmlp_mix_bias_kernel(
             src = bank[:].rearrange("p (t n) -> p n t", t=4)
             number = len(banks_done)
             banks_done.append(number)
-            if number >= FIRST_VECTOR_BANK and number % 2 == 1:
+            if number % 5 in (2, 4):
                 nc.vector.tensor_scalar_max(dst, src, 0.0)
             else:
                 nc.scalar.activation(dst, src, RELU)
@@ -156,38 +155,39 @@ def tile_list_tabmlp_mix_bias_kernel(
 
         out_hbm = out.rearrange("(m p) j -> p m j", p=P)
 
-        def output(c, block0, blocks, width, engines):
+        def output(c, block0, blocks, width, halves):
             total = blocks * BLOCK
-            stage = keep.tile([P, 2, total], F32, name=f"stage{c}_{block0}")
-            for m in range(2):
+            stage = keep.tile([P, len(halves), total], F32, name=f"stage{c}_{block0}_{halves[0][0]}")
+            for i, (m, on_scalar) in enumerate(halves):
                 acc = psum.tile([P, 4 * BLOCK], F32, name="bank")
                 rows = slice(m * P, (m + 1) * P)
                 for n in range(0, total, width):
                     cols = slice(block0 * BLOCK + n, block0 * BLOCK + n + width)
                     nc.tensor.matmul_mx(
                         out=acc[:, n : n + width],
-                        lhsT=w8[:, rows].bitcast(FP8X4),
-                        lhsT_scale=w_scales[:, 0, rows],
-                        rhs=h_codes[c, 0][:, cols].bitcast(FP8X4),
-                        rhs_scale=h_scales[c, 0][:, cols],
+                        lhsT=w4[:, 2 * m * P : 2 * (m + 1) * P].bitcast(FP4X4),
+                        lhsT_scale=w_scales[:, 1, rows],
+                        rhs=h_codes[c, 1][:, cols].bitcast(FP8X4),
+                        rhs_scale=h_scales[c, 1][:, cols],
                         start=True,
                         stop=False,
                     )
                     nc.tensor.matmul_mx(
                         out=acc[:, n : n + width],
-                        lhsT=w4[:, 2 * m * P : 2 * (m + 1) * P].bitcast(FP4X4),
-                        lhsT_scale=w_scales[:, 1, rows],
-                        rhs=h_codes[c, 1][:, cols].bitcast(FP8X4),
-                        rhs_scale=h_scales[c, 1][:, cols],
+                        lhsT=w8[:, rows].bitcast(FP8X4),
+                        lhsT_scale=w_scales[:, 0, rows],
+                        rhs=h_codes[c, 0][:, cols].bitcast(FP8X4),
+                        rhs_scale=h_scales[c, 0][:, cols],
                         start=False,
                         stop=True,
                     )
-                if engines[m] == "s":
-                    nc.scalar.activation(stage[:, m, :], acc[:, 0:total], IDENTITY, bias=bias[:, m : m + 1])
+                if on_scalar:
+                    nc.scalar.activation(stage[:, i, :], acc[:, 0:total], IDENTITY, bias=bias[:, m : m + 1])
                 else:
-                    nc.vector.tensor_scalar(stage[:, m, :], acc[:, 0:total], bias[:, m : m + 1], None, ADD)
+                    nc.vector.tensor_scalar(stage[:, i, :], acc[:, 0:total], bias[:, m : m + 1], None, ADD)
             first = c * CHUNK + block0 * BLOCK
-            nc.sync.dma_start(out_hbm[:, :, first : first + total], stage[:])
+            m0 = halves[0][0]
+            nc.sync.dma_start(out_hbm[:, m0 : m0 + len(halves), first : first + total], stage[:])
 
         gather_words(0, "x_words0")
         gather_words(1, "x_words1")
@@ -202,23 +202,28 @@ def tile_list_tabmlp_mix_bias_kernel(
         quantize_w1(1)
         hidden_chunk(1, 0)
         quantize(0, 0, 0, 4)
-        hidden_chunk(2, 0)
-        quantize(1, 0, 0, 4)
+        hidden(2, 0, 0)
+        hidden(2, 0, 1)
         hidden_chunk(0, 1)
-        quantize(2, 0, 0, 4)
+        quantize(1, 0, 0, 4)
         hidden(1, 1, 0)
         hidden(1, 1, 1)
         quantize(0, 1, 0, 4)
         hidden(1, 1, 2)
         hidden(1, 1, 3)
-        output(0, 0, 4, 512, "ss")
+        output(0, 0, 4, 512, [(0, True)])
+        output(0, 0, 4, 512, [(1, True)])
+        hidden(2, 0, 2)
+        hidden(2, 0, 3)
+        quantize(1, 1, 0, 4)
+        quantize(2, 0, 0, 4)
         hidden(2, 1, 0)
         hidden(2, 1, 1)
-        quantize(1, 1, 0, 4)
+        output(1, 0, 4, 512, [(0, True)])
         hidden(2, 1, 2)
         hidden(2, 1, 3)
-        output(1, 0, 4, 512, "ss")
+        output(1, 0, 4, 512, [(1, True)])
         quantize(2, 1, 0, 2)
-        output(2, 0, 2, 128, "sv")
+        output(2, 0, 2, 128, [(0, True), (1, False)])
         quantize(2, 1, 2, 2)
-        output(2, 2, 2, 128, "sv")
+        output(2, 2, 2, 128, [(0, True), (1, False)])

@@ -38,7 +38,7 @@ def tile_list_tabmlp_mix_bias_kernel(
     nc = tc.nc
     with ExitStack() as ctx:
         keep = ctx.enter_context(tc.tile_pool(name="keep", bufs=1))
-        psum = ctx.enter_context(tc.psum_pool(name="psum", bufs=8))
+        psum = ctx.enter_context(tc.psum_pool(name="psum", bufs=1))
 
         offsets = keep.tile([P, S // 16], U16, name="offsets")
         nc.sync.dma_start(offsets[:], offs)
@@ -116,9 +116,15 @@ def tile_list_tabmlp_mix_bias_kernel(
                 h_scales[c, g] = keep.tile([P, CHUNK], U8, name=f"h_scales{c}{g}", align_bytes=64)
 
         banks_done = []
+        banks_taken = []
+
+        def next_bank():
+            number = len(banks_taken)
+            banks_taken.append(number)
+            return psum.tile([P, 4 * BLOCK], F32, name=f"bank{number}", tag=f"bank{number % 8}")
 
         def hidden(c, g, block):
-            bank = psum.tile([P, 4 * BLOCK], F32, name="bank")
+            bank = next_bank()
             cols = slice(block * BLOCK, (block + 1) * BLOCK)
             listed = slice(c * CHUNK + block * BLOCK, c * CHUNK + (block + 1) * BLOCK)
             for t in range(4):
@@ -136,7 +142,7 @@ def tile_list_tabmlp_mix_bias_kernel(
             src = bank[:].rearrange("p (t n) -> p n t", t=4)
             number = len(banks_done)
             banks_done.append(number)
-            if number % 5 in (2, 4):
+            if number >= 5 and number % 5 in (0, 2):
                 nc.vector.tensor_scalar_max(dst, src, 0.0)
             else:
                 nc.scalar.activation(dst, src, RELU)
@@ -159,27 +165,27 @@ def tile_list_tabmlp_mix_bias_kernel(
             total = blocks * BLOCK
             stage = keep.tile([P, len(halves), total], F32, name=f"stage{c}_{block0}_{halves[0][0]}")
             for i, (m, on_scalar) in enumerate(halves):
-                acc = psum.tile([P, 4 * BLOCK], F32, name="bank")
+                acc = next_bank()
                 rows = slice(m * P, (m + 1) * P)
-                for n in range(0, total, width):
-                    cols = slice(block0 * BLOCK + n, block0 * BLOCK + n + width)
+                passes = [(1, n, width) for n in range(0, total, width)]
+                if width == total:
+                    passes = passes + [(0, 0, total)]
+                else:
+                    passes = [(0, 0, total)] + passes
+                for number, (g, n, count) in enumerate(passes):
+                    cols = slice(block0 * BLOCK + n, block0 * BLOCK + n + count)
+                    if g == 0:
+                        weights = w8[:, rows].bitcast(FP8X4)
+                    else:
+                        weights = w4[:, 2 * m * P : 2 * (m + 1) * P].bitcast(FP4X4)
                     nc.tensor.matmul_mx(
-                        out=acc[:, n : n + width],
-                        lhsT=w4[:, 2 * m * P : 2 * (m + 1) * P].bitcast(FP4X4),
-                        lhsT_scale=w_scales[:, 1, rows],
-                        rhs=h_codes[c, 1][:, cols].bitcast(FP8X4),
-                        rhs_scale=h_scales[c, 1][:, cols],
-                        start=True,
-                        stop=False,
-                    )
-                    nc.tensor.matmul_mx(
-                        out=acc[:, n : n + width],
-                        lhsT=w8[:, rows].bitcast(FP8X4),
-                        lhsT_scale=w_scales[:, 0, rows],
-                        rhs=h_codes[c, 0][:, cols].bitcast(FP8X4),
-                        rhs_scale=h_scales[c, 0][:, cols],
-                        start=False,
-                        stop=True,
+                        out=acc[:, n : n + count],
+                        lhsT=weights,
+                        lhsT_scale=w_scales[:, g, rows],
+                        rhs=h_codes[c, g][:, cols].bitcast(FP8X4),
+                        rhs_scale=h_scales[c, g][:, cols],
+                        start=number == 0,
+                        stop=number == len(passes) - 1,
                     )
                 if on_scalar:
                     nc.scalar.activation(stage[:, i, :], acc[:, 0:total], IDENTITY, bias=bias[:, m : m + 1])
@@ -202,28 +208,19 @@ def tile_list_tabmlp_mix_bias_kernel(
         quantize_w1(1)
         hidden_chunk(1, 0)
         quantize(0, 0, 0, 4)
-        hidden(2, 0, 0)
-        hidden(2, 0, 1)
         hidden_chunk(0, 1)
         quantize(1, 0, 0, 4)
-        hidden(1, 1, 0)
-        hidden(1, 1, 1)
+        hidden_chunk(1, 1)
         quantize(0, 1, 0, 4)
-        hidden(1, 1, 2)
-        hidden(1, 1, 3)
+        hidden_chunk(2, 0)
+        quantize(1, 1, 0, 4)
         output(0, 0, 4, 512, [(0, True)])
         output(0, 0, 4, 512, [(1, True)])
-        hidden(2, 0, 2)
-        hidden(2, 0, 3)
-        quantize(1, 1, 0, 4)
+        hidden_chunk(2, 1)
         quantize(2, 0, 0, 4)
-        hidden(2, 1, 0)
-        hidden(2, 1, 1)
-        output(1, 0, 4, 512, [(0, True)])
-        hidden(2, 1, 2)
-        hidden(2, 1, 3)
-        output(1, 0, 4, 512, [(1, True)])
         quantize(2, 1, 0, 2)
-        output(2, 0, 2, 128, [(0, True), (1, False)])
+        output(1, 0, 4, 512, [(0, True)])
         quantize(2, 1, 2, 2)
+        output(1, 0, 4, 512, [(1, True)])
+        output(2, 0, 2, 128, [(0, True), (1, False)])
         output(2, 2, 2, 128, [(0, True), (1, False)])

@@ -29,7 +29,7 @@ PIECE = 256
 
 
 FIRST_COLUMNS = 1024
-SCALAR_SHARE = 24
+SCALAR_SHARE = 32
 
 
 def tile_list_tabmlp_mix_bias_kernel(
@@ -41,7 +41,6 @@ def tile_list_tabmlp_mix_bias_kernel(
         psum = ctx.enter_context(tc.psum_pool(name="psum", bufs=1))
 
         offsets = keep.tile([P, S // 16], U16, name="offsets")
-        nc.sync.dma_start(offsets[:], offs)
 
         table_words = keep.tile([P, T], I32, name="table_words", align_bytes=64)
         table_scales = keep.tile([P, T], U8, name="table_scales", align_bytes=64)
@@ -49,6 +48,7 @@ def tile_list_tabmlp_mix_bias_kernel(
         scales_hbm = tab[0, 512 * T : 528 * T].rearrange("(q r t) -> r q t", q=4, r=4).bitcast(I32)
         nc.vector.memset(table_scales[:].bitcast(I32), 0)
         nc.sync.dma_start(table_words[:, 0:FIRST_COLUMNS], words_hbm[:, 0:FIRST_COLUMNS])
+        nc.sync.dma_start(offsets[:], offs)
         for r in range(4):
             nc.sync.dma_start(table_scales[r:P:32, :].bitcast(I32), scales_hbm[r])
         nc.sync.dma_start(table_words[:, FIRST_COLUMNS:T], words_hbm[:, FIRST_COLUMNS:T])
@@ -142,10 +142,24 @@ def tile_list_tabmlp_mix_bias_kernel(
             src = bank[:].rearrange("p (t n) -> p n t", t=4)
             number = len(banks_done)
             banks_done.append(number)
-            if number >= 5 and number % 5 in (0, 2):
+            if number >= 4 and number % 3 == 1:
                 nc.vector.tensor_scalar_max(dst, src, 0.0)
             else:
                 nc.scalar.activation(dst, src, RELU)
+
+        def warm(c, count):
+            bank = next_bank()
+            first = c * CHUNK
+            for repeat in range(count):
+                nc.tensor.matmul_mx(
+                    out=bank[:],
+                    lhsT=x_words[c][:, 0:P].bitcast(FP8X4),
+                    lhsT_scale=x_scales[:, first : first + P],
+                    rhs=x_words[c][:].bitcast(FP8X4),
+                    rhs_scale=x_scales[:, first : first + CHUNK],
+                    start=True,
+                    stop=True,
+                )
 
         def hidden_chunk(c, g):
             for block in range(BLOCKS):
@@ -197,6 +211,7 @@ def tile_list_tabmlp_mix_bias_kernel(
 
         gather_words(0, "x_words0")
         gather_words(1, "x_words1")
+        warm(1, 2)
         convert(0, 0, PIECE // 4, True)
         convert(1, 0, SCALAR_SHARE, True)
         convert(1, SCALAR_SHARE, PIECE // 4, False)
@@ -214,13 +229,16 @@ def tile_list_tabmlp_mix_bias_kernel(
         quantize(0, 1, 0, 4)
         hidden_chunk(2, 0)
         quantize(1, 1, 0, 4)
-        output(0, 0, 4, 512, [(0, True)])
+        output(0, 0, 4, 512, [(0, False)])
+        hidden(2, 1, 0)
+        hidden(2, 1, 1)
         output(0, 0, 4, 512, [(1, True)])
-        hidden_chunk(2, 1)
+        hidden(2, 1, 2)
+        hidden(2, 1, 3)
         quantize(2, 0, 0, 4)
         quantize(2, 1, 0, 2)
-        output(1, 0, 4, 512, [(0, True)])
         quantize(2, 1, 2, 2)
+        output(1, 0, 4, 512, [(0, True)])
         output(1, 0, 4, 512, [(1, True)])
         output(2, 0, 2, 128, [(0, True), (1, False)])
         output(2, 2, 2, 128, [(0, True), (1, False)])

@@ -28,8 +28,8 @@ GROUPS = H // GROUP
 PIECE = 256
 
 
-FIRST_COLUMNS = 1024
-SCALAR_SHARE = 32
+FIRST_COLUMNS = 512
+SCALAR_SHARE = 24
 
 
 def tile_list_tabmlp_mix_bias_kernel(
@@ -47,7 +47,9 @@ def tile_list_tabmlp_mix_bias_kernel(
         words_hbm = tab[0, 0 : 512 * T].rearrange("(p c) -> p c", p=P).bitcast(I32)
         scales_hbm = tab[0, 512 * T : 528 * T].rearrange("(q r t) -> r q t", q=4, r=4).bitcast(I32)
         nc.vector.memset(table_scales[:].bitcast(I32), 0)
-        nc.sync.dma_start(table_words[:, 0:FIRST_COLUMNS], words_hbm[:, 0:FIRST_COLUMNS])
+        for first in range(0, FIRST_COLUMNS, FIRST_COLUMNS // 2):
+            cols = slice(first, first + FIRST_COLUMNS // 2)
+            nc.sync.dma_start(table_words[:, cols], words_hbm[:, cols])
         nc.sync.dma_start(offsets[:], offs)
         for r in range(4):
             nc.sync.dma_start(table_scales[r:P:32, :].bitcast(I32), scales_hbm[r])

@@ -45,22 +45,33 @@ def tile_list_tabmlp_mix_bias_kernel(
         table_words = keep.tile([P, T], I32, name="table_words", align_bytes=64)
         table_scales = keep.tile([P, T], U8, name="table_scales", align_bytes=64)
         words_hbm = tab[0, 0 : 512 * T].rearrange("(p c) -> p c", p=P).bitcast(I32)
-        scales_hbm = tab[0, 512 * T : 528 * T].rearrange("(q r t) -> r q t", q=4, r=4).bitcast(I32)
+        scales_hbm = tab[0, 512 * T : 528 * T].rearrange("(q t) -> q t", q=16).bitcast(I32)
         nc.vector.memset(table_scales[:].bitcast(I32), 0)
         for first in range(0, FIRST_COLUMNS, FIRST_COLUMNS // 2):
             cols = slice(first, first + FIRST_COLUMNS // 2)
             nc.sync.dma_start(table_words[:, cols], words_hbm[:, cols])
         nc.sync.dma_start(offsets[:], offs)
-        for r in range(4):
-            nc.sync.dma_start(table_scales[r:P:32, :].bitcast(I32), scales_hbm[r])
+        nc.sync.dma_start(table_scales[4:P:8, :].bitcast(I32), scales_hbm)
         nc.sync.dma_start(table_words[:, FIRST_COLUMNS:T], words_hbm[:, FIRST_COLUMNS:T])
 
         w1_hbm = w1.rearrange("(p j) c -> p j c", j=4)
         w1_raw = []
-        for piece in range(H // PIECE):
-            raw = keep.tile([P, 4, PIECE], F32, name=f"w1_raw{piece}")
-            nc.sync.dma_start(raw[:], w1_hbm[:, :, piece * PIECE : (piece + 1) * PIECE])
-            w1_raw.append(raw)
+
+        def load_w1(pieces):
+            for piece in pieces:
+                raw = keep.tile([P, 4, PIECE], F32, name=f"w1_raw{piece}")
+                nc.sync.dma_start(raw[:], w1_hbm[:, :, piece * PIECE : (piece + 1) * PIECE])
+                w1_raw.append(raw)
+
+        load_w1(range(3))
+        x_scales = keep.tile([P, S], U8, name="x_scales", align_bytes=64)
+        nc.vector.memset(x_scales[:].bitcast(I32), 0)
+        picked_scales = keep.tile([P, S], U8, name="picked_scales", align_bytes=64)
+        nc.vector.tensor_copy(picked_scales[:], table_scales[:].indirect(offsets[:]))
+        for r in range(4):
+            nc.sync.dma_start(x_scales[r:P:32, :].bitcast(I32), picked_scales[8 * r + 4 : P : 32, :].bitcast(I32))
+
+        load_w1(range(3, H // PIECE))
 
         w8 = keep.tile([P, M], I32, name="w8", align_bytes=64)
         nc.sync.dma_start(w8[:], w8_words[0].rearrange("p n i -> p (n i)").bitcast(I32))
@@ -75,9 +86,6 @@ def tile_list_tabmlp_mix_bias_kernel(
                 nc.sync.dma_start(w_scales[r:P:32, g, :].bitcast(I32), rows[r])
         bias = keep.tile([P, 2], F32, name="bias")
         nc.sync.dma_start(bias[:], b.rearrange("(m p) -> p m", p=P))
-
-        x_scales = keep.tile([P, S], U8, name="x_scales", align_bytes=64)
-        nc.vector.tensor_copy(x_scales[:], table_scales[:].indirect(offsets[:]))
 
         x_words = {}
 
@@ -156,9 +164,9 @@ def tile_list_tabmlp_mix_bias_kernel(
                 nc.tensor.matmul_mx(
                     out=bank[:],
                     lhsT=x_words[c][:, 0:P].bitcast(FP8X4),
-                    lhsT_scale=x_scales[:, first : first + P],
+                    lhsT_scale=picked_scales[:, first : first + P],
                     rhs=x_words[c][:].bitcast(FP8X4),
-                    rhs_scale=x_scales[:, first : first + CHUNK],
+                    rhs_scale=picked_scales[:, first : first + CHUNK],
                     start=True,
                     stop=True,
                 )

@@ -28,8 +28,8 @@ GROUPS = H // GROUP
 PIECE = 256
 
 
-FIRST_COLUMNS = 512
-SCALAR_SHARE = 24
+FIRST_COLUMNS = 768
+SCALAR_SHARE = 32
 
 
 def tile_list_tabmlp_mix_bias_kernel(
@@ -51,7 +51,7 @@ def tile_list_tabmlp_mix_bias_kernel(
             cols = slice(first, first + FIRST_COLUMNS // 2)
             nc.sync.dma_start(table_words[:, cols], words_hbm[:, cols])
         nc.sync.dma_start(offsets[:], offs)
-        nc.sync.dma_start(table_scales[4:P:8, :].bitcast(I32), scales_hbm)
+        nc.sync.dma_start(table_scales[32:96:4, :].bitcast(I32), scales_hbm)
         nc.sync.dma_start(table_words[:, FIRST_COLUMNS:T], words_hbm[:, FIRST_COLUMNS:T])
 
         w1_hbm = w1.rearrange("(p j) c -> p j c", j=4)
@@ -69,7 +69,7 @@ def tile_list_tabmlp_mix_bias_kernel(
         picked_scales = keep.tile([P, S], U8, name="picked_scales", align_bytes=64)
         nc.vector.tensor_copy(picked_scales[:], table_scales[:].indirect(offsets[:]))
         for r in range(4):
-            nc.sync.dma_start(x_scales[r:P:32, :].bitcast(I32), picked_scales[8 * r + 4 : P : 32, :].bitcast(I32))
+            nc.sync.dma_start(x_scales[r:P:32, :].bitcast(I32), picked_scales[32 + 4 * r : 96 : 16, :].bitcast(I32))
 
         load_w1(range(3, H // PIECE))
 

@@ -42,8 +42,8 @@ def tile_list_tabmlp_mix_bias_kernel(
 
         offsets = keep.tile([P, S // 16], U16, name="offsets")
 
-        table_words = keep.tile([P, T], I32, name="table_words", align_bytes=64)
-        table_scales = keep.tile([P, T], U8, name="table_scales", align_bytes=64)
+        table_words = keep.tile([P, T], I32, name="table_words", align_bytes=256)
+        table_scales = keep.tile([P, T], U8, name="table_scales", align_bytes=256)
         words_hbm = tab[0, 0 : 512 * T].rearrange("(p c) -> p c", p=P).bitcast(I32)
         scales_hbm = tab[0, 512 * T : 528 * T].rearrange("(q t) -> q t", q=16).bitcast(I32)
         nc.vector.memset(table_scales[:].bitcast(I32), 0)
@@ -64,21 +64,21 @@ def tile_list_tabmlp_mix_bias_kernel(
                 w1_raw.append(raw)
 
         load_w1(range(3))
-        x_scales = keep.tile([P, S], U8, name="x_scales", align_bytes=64)
+        x_scales = keep.tile([P, S], U8, name="x_scales", align_bytes=256)
         nc.vector.memset(x_scales[:].bitcast(I32), 0)
-        picked_scales = keep.tile([P, S], U8, name="picked_scales", align_bytes=64)
+        picked_scales = keep.tile([P, S], U8, name="picked_scales", align_bytes=256)
         nc.vector.tensor_copy(picked_scales[:], table_scales[:].indirect(offsets[:]))
         for r in range(4):
             nc.sync.dma_start(x_scales[r:P:32, :].bitcast(I32), picked_scales[32 + 4 * r : 96 : 16, :].bitcast(I32))
 
         load_w1(range(3, H // PIECE))
 
-        w8 = keep.tile([P, M], I32, name="w8", align_bytes=64)
+        w8 = keep.tile([P, M], I32, name="w8", align_bytes=256)
         nc.sync.dma_start(w8[:], w8_words[0].rearrange("p n i -> p (n i)").bitcast(I32))
-        w4 = keep.tile([P, 2 * M], U8, name="w4", align_bytes=64)
+        w4 = keep.tile([P, 2 * M], U8, name="w4", align_bytes=256)
         nc.sync.dma_start(w4[:].bitcast(I32), w4_words[0].bitcast(I32))
 
-        w_scales = keep.tile([P, 2, M], U8, name="w_scales", align_bytes=64)
+        w_scales = keep.tile([P, 2, M], U8, name="w_scales", align_bytes=256)
         nc.vector.memset(w_scales[:].rearrange("p g n -> p (g n)").bitcast(I32), 0)
         for g, src in enumerate((w8_scales, w4_scales)):
             rows = src[0].rearrange("(q r) n -> r q n", r=4).bitcast(I32)
@@ -90,7 +90,7 @@ def tile_list_tabmlp_mix_bias_kernel(
         x_words = {}
 
         def gather_words(c, tag):
-            words = keep.tile([P, CHUNK], U32, name=f"x_words{c}", tag=tag, align_bytes=64)
+            words = keep.tile([P, CHUNK], U32, name=f"x_words{c}", tag=tag, align_bytes=256)
             listed = offsets[:, c * (CHUNK // 16) : (c + 1) * (CHUNK // 16)]
             nc.vector.tensor_copy(words[:], table_words[:].bitcast(U32).indirect(listed))
             x_words[c] = words
@@ -99,9 +99,9 @@ def tile_list_tabmlp_mix_bias_kernel(
         w1_codes = {}
         w1_scales = {}
         for g in range(GROUPS):
-            w1_grouped[g] = keep.tile([P, 4 * GROUP], BF16, name=f"w1_grouped{g}", tag=f"w1_grouped{g}", align_bytes=64)
-            w1_codes[g] = keep.tile([P, GROUP], U32, name=f"w1_codes{g}", align_bytes=64)
-            w1_scales[g] = keep.tile([P, GROUP], U8, name=f"w1_scales{g}", align_bytes=64)
+            w1_grouped[g] = keep.tile([P, 4 * GROUP], BF16, name=f"w1_grouped{g}", tag=f"w1_grouped{g}", align_bytes=256)
+            w1_codes[g] = keep.tile([P, GROUP], U32, name=f"w1_codes{g}", align_bytes=256)
+            w1_scales[g] = keep.tile([P, GROUP], U8, name=f"w1_scales{g}", align_bytes=256)
 
         def convert(piece, first, last, on_scalar):
             g, i = divmod(piece, GROUP // PIECE)
@@ -121,9 +121,9 @@ def tile_list_tabmlp_mix_bias_kernel(
         h_scales = {}
         for c in range(CHUNKS):
             for g in range(GROUPS):
-                h_grouped[c, g] = keep.tile([P, 4 * CHUNK], BF16, name=f"h_grouped{c}{g}", align_bytes=64)
-                h_codes[c, g] = keep.tile([P, CHUNK], U32, name=f"h_codes{c}{g}", align_bytes=64)
-                h_scales[c, g] = keep.tile([P, CHUNK], U8, name=f"h_scales{c}{g}", align_bytes=64)
+                h_grouped[c, g] = keep.tile([P, 4 * CHUNK], BF16, name=f"h_grouped{c}{g}", align_bytes=256)
+                h_codes[c, g] = keep.tile([P, CHUNK], U32, name=f"h_codes{c}{g}", align_bytes=256)
+                h_scales[c, g] = keep.tile([P, CHUNK], U8, name=f"h_scales{c}{g}", align_bytes=256)
 
         banks_done = []
         banks_taken = []

@@ -157,16 +157,16 @@ def tile_list_tabmlp_mix_bias_kernel(
             else:
                 nc.scalar.activation(dst, src, RELU)
 
-        def warm(c, count):
+        def warm(c, widths):
             bank = next_bank()
             first = c * CHUNK
-            for repeat in range(count):
+            for width in widths:
                 nc.tensor.matmul_mx(
-                    out=bank[:],
+                    out=bank[:, 0:width],
                     lhsT=x_words[c][:, 0:P].bitcast(FP8X4),
                     lhsT_scale=picked_scales[:, first : first + P],
-                    rhs=x_words[c][:].bitcast(FP8X4),
-                    rhs_scale=picked_scales[:, first : first + CHUNK],
+                    rhs=x_words[c][:, 0:width].bitcast(FP8X4),
+                    rhs_scale=picked_scales[:, first : first + width],
                     start=True,
                     stop=True,
                 )
@@ -220,8 +220,8 @@ def tile_list_tabmlp_mix_bias_kernel(
             nc.sync.dma_start(out_hbm[:, m0 : m0 + len(halves), first : first + total], stage[:])
 
         gather_words(0, "x_words0")
+        warm(0, [CHUNK, CHUNK, CHUNK, CHUNK // 2])
         gather_words(1, "x_words1")
-        warm(1, 2)
         convert(0, 0, PIECE // 4, True)
         convert(1, 0, SCALAR_SHARE, True)
         convert(1, SCALAR_SHARE, PIECE // 4, False)

@@ -30,6 +30,8 @@ PIECE = 256
 
 FIRST_COLUMNS = 768
 SCALAR_SHARE = 32
+SCALAR_SHARE_THIRD = 64
+LAG = 3
 
 
 def tile_list_tabmlp_mix_bias_kernel(
@@ -152,7 +154,7 @@ def tile_list_tabmlp_mix_bias_kernel(
             src = bank[:].rearrange("p (t n) -> p n t", t=4)
             number = len(banks_done)
             banks_done.append(number)
-            if number >= 4 and number % 3 == 1:
+            if number % 3 == 2:
                 nc.vector.tensor_scalar_max(dst, src, 0.0)
             else:
                 nc.scalar.activation(dst, src, RELU)
@@ -170,10 +172,6 @@ def tile_list_tabmlp_mix_bias_kernel(
                     start=True,
                     stop=True,
                 )
-
-        def hidden_chunk(c, g):
-            for block in range(BLOCKS):
-                hidden(c, g, block)
 
         def quantize(c, g, block0, blocks):
             cols = slice(block0 * BLOCK, (block0 + blocks) * BLOCK)
@@ -227,27 +225,29 @@ def tile_list_tabmlp_mix_bias_kernel(
         convert(1, SCALAR_SHARE, PIECE // 4, False)
         quantize_w1(0)
         gather_words(2, "w1_grouped0")
-        convert(2, 0, PIECE // 4, True)
-        hidden_chunk(0, 0)
+        convert(2, 0, SCALAR_SHARE_THIRD, True)
         convert(3, 0, PIECE // 4, False)
-        quantize_w1(1)
-        hidden_chunk(1, 0)
-        quantize(0, 0, 0, 4)
-        hidden_chunk(0, 1)
-        quantize(1, 0, 0, 4)
-        hidden_chunk(1, 1)
-        quantize(0, 1, 0, 4)
-        hidden_chunk(2, 0)
-        quantize(1, 1, 0, 4)
-        output(0, 0, 4, 512, [(0, False)])
-        hidden(2, 1, 0)
-        hidden(2, 1, 1)
-        output(0, 0, 4, 512, [(1, True)])
-        hidden(2, 1, 2)
-        hidden(2, 1, 3)
-        quantize(2, 0, 0, 4)
-        quantize(2, 1, 0, 2)
-        quantize(2, 1, 2, 2)
+
+        runs = [(0, 0, 0, 4), (1, 0, 0, 4), (2, 0, 0, 2), (0, 1, 0, 4), (1, 1, 0, 4), (2, 1, 0, 2), (2, 0, 2, 2), (2, 1, 2, 2)]
+        steps = [(c, g, block) for c, g, block0, blocks in runs for block in range(block0, block0 + blocks)]
+        due = {}
+        end = 0
+        for run in runs:
+            end = end + run[3]
+            due[end - 1 + LAG] = run
+        for number, (c, g, block) in enumerate(steps):
+            if number == BLOCKS:
+                quantize_w1(1)
+            hidden(c, g, block)
+            if number in due:
+                quantize(*due[number])
+            if number == len(steps) - 3:
+                output(0, 0, 4, 512, [(0, False)])
+            if number == len(steps) - 2:
+                output(0, 0, 4, 512, [(1, True)])
+        for number in sorted(due):
+            if number >= len(steps):
+                quantize(*due[number])
         output(1, 0, 4, 512, [(0, True)])
         output(1, 0, 4, 512, [(1, True)])
         output(2, 0, 2, 128, [(0, True), (1, False)])

@@ -154,7 +154,7 @@ def tile_list_tabmlp_mix_bias_kernel(
             src = bank[:].rearrange("p (t n) -> p n t", t=4)
             number = len(banks_done)
             banks_done.append(number)
-            if number % 3 == 2:
+            if number in (1, 3, 5) or number > 8 and number % 3 == 2:
                 nc.vector.tensor_scalar_max(dst, src, 0.0)
             else:
                 nc.scalar.activation(dst, src, RELU)
@@ -226,7 +226,10 @@ def tile_list_tabmlp_mix_bias_kernel(
         quantize_w1(0)
         gather_words(2, "w1_grouped0")
         convert(2, 0, SCALAR_SHARE_THIRD, True)
-        convert(3, 0, PIECE // 4, False)
+        order = w1_grouped[1][:].rearrange("p (t m j) -> p m t j", t=4, j=4)
+        nc.gpsimd.tensor_scalar(
+            order[:, PIECE // 4 : PIECE // 2, :, :], w1_raw[3][:].rearrange("p j (m t) -> p m t j", t=4), 1.0, 0.0, MULT, ADD
+        )
 
         runs = [(0, 0, 0, 4), (1, 0, 0, 4), (2, 0, 0, 2), (0, 1, 0, 4), (1, 1, 0, 4), (2, 1, 0, 2), (2, 0, 2, 2), (2, 1, 2, 2)]
         steps = [(c, g, block) for c, g, block0, blocks in runs for block in range(block0, block0 + blocks)]

@@ -42,7 +42,7 @@ def tile_list_tabmlp_mix_bias_kernel(
         keep = ctx.enter_context(tc.tile_pool(name="keep", bufs=1))
         psum = ctx.enter_context(tc.psum_pool(name="psum", bufs=1))
 
-        offsets = keep.tile([P, S // 16], U16, name="offsets")
+        offsets = keep.tile([P, S // 16], U16, name="offsets", align_bytes=256)
 
         table_words = keep.tile([P, T], I32, name="table_words", align_bytes=256)
         table_scales = keep.tile([P, T], U8, name="table_scales", align_bytes=256)
@@ -61,7 +61,7 @@ def tile_list_tabmlp_mix_bias_kernel(
 
         def load_w1(pieces):
             for piece in pieces:
-                raw = keep.tile([P, 4, PIECE], F32, name=f"w1_raw{piece}")
+                raw = keep.tile([P, 4, PIECE], F32, name=f"w1_raw{piece}", align_bytes=256)
                 nc.sync.dma_start(raw[:], w1_hbm[:, :, piece * PIECE : (piece + 1) * PIECE])
                 w1_raw.append(raw)
 
@@ -86,7 +86,7 @@ def tile_list_tabmlp_mix_bias_kernel(
             rows = src[0].rearrange("(q r) n -> r q n", r=4).bitcast(I32)
             for r in range(4):
                 nc.sync.dma_start(w_scales[r:P:32, g, :].bitcast(I32), rows[r])
-        bias = keep.tile([P, 2], F32, name="bias")
+        bias = keep.tile([P, 2], F32, name="bias", align_bytes=256)
         nc.sync.dma_start(bias[:], b.rearrange("(m p) -> p m", p=P))
 
         x_words = {}
@@ -185,7 +185,7 @@ def tile_list_tabmlp_mix_bias_kernel(
 
         def output(c, block0, blocks, width, halves):
             total = blocks * BLOCK
-            stage = keep.tile([P, len(halves), total], F32, name=f"stage{c}_{block0}_{halves[0][0]}")
+            stage = keep.tile([P, len(halves), total], F32, name=f"stage{c}_{block0}_{halves[0][0]}", align_bytes=256)
             for i, (m, on_scalar) in enumerate(halves):
                 acc = next_bank()
                 rows = slice(m * P, (m + 1) * P)

@@ -25,12 +25,11 @@ GROUP = 512
 CHUNKS = S // CHUNK
 BLOCKS = CHUNK // BLOCK
 GROUPS = H // GROUP
-PIECE = 256
+WIDTHS = (128, 128, 128, 128, 256, 256)
 
 
 FIRST_COLUMNS = 768
-SCALAR_SHARE = 32
-SCALAR_SHARE_THIRD = 64
+SCALAR_SHARE = 20
 LAG = 3
 
 
@@ -61,11 +60,12 @@ def tile_list_tabmlp_mix_bias_kernel(
 
         def load_w1(pieces):
             for piece in pieces:
-                raw = keep.tile([P, 4, PIECE], F32, name=f"w1_raw{piece}", align_bytes=256)
-                nc.sync.dma_start(raw[:], w1_hbm[:, :, piece * PIECE : (piece + 1) * PIECE])
+                start = sum(WIDTHS[:piece])
+                raw = keep.tile([P, 4, WIDTHS[piece]], F32, name=f"w1_raw{piece}", align_bytes=256)
+                nc.sync.dma_start(raw[:], w1_hbm[:, :, start : start + WIDTHS[piece]])
                 w1_raw.append(raw)
 
-        load_w1(range(3))
+        load_w1(range(len(WIDTHS) - 1))
         x_scales = keep.tile([P, S], U8, name="x_scales", align_bytes=256)
         nc.vector.memset(x_scales[:].bitcast(I32), 0)
         picked_scales = keep.tile([P, S], U8, name="picked_scales", align_bytes=256)
@@ -73,7 +73,7 @@ def tile_list_tabmlp_mix_bias_kernel(
         for r in range(4):
             nc.sync.dma_start(x_scales[r:P:32, :].bitcast(I32), picked_scales[32 + 4 * r : 96 : 16, :].bitcast(I32))
 
-        load_w1(range(3, H // PIECE))
+        load_w1([len(WIDTHS) - 1])
 
         w8 = keep.tile([P, M], I32, name="w8", align_bytes=256)
         nc.sync.dma_start(w8[:], w8_words[0].rearrange("p n i -> p (n i)").bitcast(I32))
@@ -106,9 +106,9 @@ def tile_list_tabmlp_mix_bias_kernel(
             w1_scales[g] = keep.tile([P, GROUP], U8, name=f"w1_scales{g}", align_bytes=256)
 
         def convert(piece, first, last, on_scalar):
-            g, i = divmod(piece, GROUP // PIECE)
+            g, start = divmod(sum(WIDTHS[:piece]), GROUP)
             order = w1_grouped[g][:].rearrange("p (t m j) -> p m j t", t=4, j=4)
-            dst = order[:, i * PIECE // 4 + first : i * PIECE // 4 + last, :, :]
+            dst = order[:, start // 4 + first : start // 4 + last, :, :]
             src = w1_raw[piece][:].rearrange("p j (m t) -> p m j t", t=4)[:, first:last, :, :]
             if on_scalar:
                 nc.scalar.copy(dst, src)
@@ -220,15 +220,16 @@ def tile_list_tabmlp_mix_bias_kernel(
         gather_words(0, "x_words0")
         warm(0, [CHUNK, CHUNK, CHUNK, CHUNK // 2])
         gather_words(1, "x_words1")
-        convert(0, 0, PIECE // 4, True)
-        convert(1, 0, SCALAR_SHARE, True)
-        convert(1, SCALAR_SHARE, PIECE // 4, False)
+        for piece in range(3):
+            convert(piece, 0, WIDTHS[piece] // 4, True)
+        convert(3, 0, SCALAR_SHARE, True)
+        convert(3, SCALAR_SHARE, WIDTHS[3] // 4, False)
         quantize_w1(0)
         gather_words(2, "w1_grouped0")
-        convert(2, 0, SCALAR_SHARE_THIRD, True)
+        convert(4, 0, WIDTHS[4] // 4, True)
         order = w1_grouped[1][:].rearrange("p (t m j) -> p m t j", t=4, j=4)
         nc.gpsimd.tensor_scalar(
-            order[:, PIECE // 4 : PIECE // 2, :, :], w1_raw[3][:].rearrange("p j (m t) -> p m t j", t=4), 1.0, 0.0, MULT, ADD
+            order[:, WIDTHS[4] // 4 : GROUP // 4, :, :], w1_raw[5][:].rearrange("p j (m t) -> p m t j", t=4), 1.0, 0.0, MULT, ADD
         )
 
         runs = [(0, 0, 0, 4), (1, 0, 0, 4), (2, 0, 0, 2), (0, 1, 0, 4), (1, 1, 0, 4), (2, 1, 0, 2), (2, 0, 2, 2), (2, 1, 2, 2)]

@@ -19,18 +19,23 @@ ADD = mybir.AluOpType.add
 MULT = mybir.AluOpType.mult
 
 P = 128
-CHUNK = 512
+ALIGN = 256
+BANKS = 8
 BLOCK = 128
+CHUNK = 512
 GROUP = 512
-CHUNKS = S // CHUNK
-BLOCKS = CHUNK // BLOCK
-GROUPS = H // GROUP
-WIDTHS = (128, 128, 128, 128, 256, 256)
-
-
+BLOCKS = S // BLOCK
+PART_BLOCKS = (2, 2, 2, 2, 2, 2)
+PARTS = len(PART_BLOCKS)
+WIDTHS = (128, 128, 128, 128, 128, 96, 288)
+GATHERS = (512, 512, 256, 256)
 FIRST_COLUMNS = 768
-SCALAR_SHARE = 20
-LAG = 3
+VECTOR_SHARE = 12
+PLACES = dict(
+    [("h_grouped0_4", 0), ("w_rows", 1792), ("w1_scales1", 2048), ("h_grouped0_5", 2560), ("w1_grouped1", 4608)]
+    + [(f"h_scales0_{part}", 4608 + 256 * part) for part in range(6)]
+)
+WARM_WIDTHS = (512, 512, 512, 256)
 
 
 def tile_list_tabmlp_mix_bias_kernel(
@@ -39,220 +44,280 @@ def tile_list_tabmlp_mix_bias_kernel(
     nc = tc.nc
     with ExitStack() as ctx:
         keep = ctx.enter_context(tc.tile_pool(name="keep", bufs=1))
+        shared = ctx.enter_context(tc.tile_pool(name="shared", bufs=1))
         psum = ctx.enter_context(tc.psum_pool(name="psum", bufs=1))
 
-        offsets = keep.tile([P, S // 16], U16, name="offsets", align_bytes=256)
+        def sbuf(shape, dtype, name, slot=None):
+            if name in PLACES:
+                return shared.tile(shape, dtype, name=name, offset=PLACES[name], align_bytes=ALIGN)
+            return keep.tile(shape, dtype, name=name, tag=slot or name, align_bytes=ALIGN)
 
-        table_words = keep.tile([P, T], I32, name="table_words", align_bytes=256)
-        table_scales = keep.tile([P, T], U8, name="table_scales", align_bytes=256)
+        offsets = sbuf([P, S // 16], U16, "offsets")
+        table_words = sbuf([P, T], I32, "table_words")
+        table_scales = sbuf([P, T], U8, "table_scales")
         words_hbm = tab[0, 0 : 512 * T].rearrange("(p c) -> p c", p=P).bitcast(I32)
         scales_hbm = tab[0, 512 * T : 528 * T].rearrange("(q t) -> q t", q=16).bitcast(I32)
         nc.vector.memset(table_scales[:].bitcast(I32), 0)
-        for first in range(0, FIRST_COLUMNS, FIRST_COLUMNS // 2):
-            cols = slice(first, first + FIRST_COLUMNS // 2)
-            nc.sync.dma_start(table_words[:, cols], words_hbm[:, cols])
+        nc.sync.dma_start(table_words[:, 0:FIRST_COLUMNS], words_hbm[:, 0:FIRST_COLUMNS])
         nc.sync.dma_start(offsets[:], offs)
+        w_rows = sbuf([P, 2, 2 * M], U8, "w_rows")
+        for g, src in enumerate((w8_scales, w4_scales)):
+            nc.sync.dma_start(w_rows[32:96:4, g, 0:M].bitcast(I32), src[0].bitcast(I32))
         nc.sync.dma_start(table_scales[32:96:4, :].bitcast(I32), scales_hbm)
         nc.sync.dma_start(table_words[:, FIRST_COLUMNS:T], words_hbm[:, FIRST_COLUMNS:T])
 
         w1_hbm = w1.rearrange("(p j) c -> p j c", j=4)
-        w1_raw = []
+        w1_raw = {}
 
-        def load_w1(pieces):
-            for piece in pieces:
-                start = sum(WIDTHS[:piece])
-                raw = keep.tile([P, 4, WIDTHS[piece]], F32, name=f"w1_raw{piece}", align_bytes=256)
-                nc.sync.dma_start(raw[:], w1_hbm[:, :, start : start + WIDTHS[piece]])
-                w1_raw.append(raw)
+        def load_w1(piece):
+            start = sum(WIDTHS[:piece])
+            w1_raw[piece] = sbuf([P, 4, WIDTHS[piece]], F32, f"w1_raw{piece}")
+            nc.sync.dma_start(w1_raw[piece][:], w1_hbm[:, :, start : start + WIDTHS[piece]])
 
-        load_w1(range(len(WIDTHS) - 1))
-        x_scales = keep.tile([P, S], U8, name="x_scales", align_bytes=256)
+        for piece in range(5):
+            load_w1(piece)
+        x_scales = sbuf([P, S], U8, "x_scales")
         nc.vector.memset(x_scales[:].bitcast(I32), 0)
-        picked_scales = keep.tile([P, S], U8, name="picked_scales", align_bytes=256)
+        picked_scales = sbuf([P, S], U8, "picked_scales")
         nc.vector.tensor_copy(picked_scales[:], table_scales[:].indirect(offsets[:]))
         for r in range(4):
             nc.sync.dma_start(x_scales[r:P:32, :].bitcast(I32), picked_scales[32 + 4 * r : 96 : 16, :].bitcast(I32))
+        for piece in range(5, len(WIDTHS)):
+            load_w1(piece)
 
-        load_w1([len(WIDTHS) - 1])
-
-        w8 = keep.tile([P, M], I32, name="w8", align_bytes=256)
+        w8 = sbuf([P, M], I32, "w8")
         nc.sync.dma_start(w8[:], w8_words[0].rearrange("p n i -> p (n i)").bitcast(I32))
-        w4 = keep.tile([P, 2 * M], U8, name="w4", align_bytes=256)
+        w4 = sbuf([P, 2 * M], U8, "w4")
         nc.sync.dma_start(w4[:].bitcast(I32), w4_words[0].bitcast(I32))
-
-        w_scales = keep.tile([P, 2, M], U8, name="w_scales", align_bytes=256)
+        w_scales = sbuf([P, 2, M], U8, "w_scales")
         nc.vector.memset(w_scales[:].rearrange("p g n -> p (g n)").bitcast(I32), 0)
-        for g, src in enumerate((w8_scales, w4_scales)):
-            rows = src[0].rearrange("(q r) n -> r q n", r=4).bitcast(I32)
-            for r in range(4):
-                nc.sync.dma_start(w_scales[r:P:32, g, :].bitcast(I32), rows[r])
-        bias = keep.tile([P, 2], F32, name="bias", align_bytes=256)
+        for r in range(4):
+            rows = w_rows[32 + 4 * r : 96 : 16, :, 0:M]
+            nc.sync.dma_start(w_scales[r:P:32, :, :].bitcast(I32), rows.bitcast(I32))
+        bias = sbuf([P, 2], F32, "bias")
         nc.sync.dma_start(bias[:], b.rearrange("(m p) -> p m", p=P))
 
         x_words = {}
 
-        def gather_words(c, tag):
-            words = keep.tile([P, CHUNK], U32, name=f"x_words{c}", tag=tag, align_bytes=256)
-            listed = offsets[:, c * (CHUNK // 16) : (c + 1) * (CHUNK // 16)]
+        def gather(number, slot=None):
+            first = sum(GATHERS[:number])
+            count = GATHERS[number]
+            words = sbuf([P, count], U32, f"x_words{number}", slot)
+            listed = offsets[:, first // 16 : (first + count) // 16]
             nc.vector.tensor_copy(words[:], table_words[:].bitcast(U32).indirect(listed))
-            x_words[c] = words
+            for start in range(0, count, BLOCK):
+                x_words[(first + start) // BLOCK] = words[:, start : start + BLOCK]
+            return words
 
-        w1_grouped = {}
-        w1_codes = {}
-        w1_scales = {}
-        for g in range(GROUPS):
-            w1_grouped[g] = keep.tile([P, 4 * GROUP], BF16, name=f"w1_grouped{g}", tag=f"w1_grouped{g}", align_bytes=256)
-            w1_codes[g] = keep.tile([P, GROUP], U32, name=f"w1_codes{g}", align_bytes=256)
-            w1_scales[g] = keep.tile([P, GROUP], U8, name=f"w1_scales{g}", align_bytes=256)
+        w1_grouped = [sbuf([P, 4 * GROUP], BF16, f"w1_grouped{g}") for g in range(2)]
+        w1_codes = [sbuf([P, GROUP], U32, f"w1_codes{g}") for g in range(2)]
+        w1_scales = [sbuf([P, GROUP], U8, f"w1_scales{g}") for g in range(2)]
 
-        def convert(piece, first, last, on_scalar):
+        def convert(piece, first, last, engine):
             g, start = divmod(sum(WIDTHS[:piece]), GROUP)
-            order = w1_grouped[g][:].rearrange("p (t m j) -> p m j t", t=4, j=4)
-            dst = order[:, start // 4 + first : start // 4 + last, :, :]
+            quads = slice(start // 4 + first, start // 4 + last)
+            if engine == "gpsimd":
+                dst = w1_grouped[g][:].rearrange("p (t m j) -> p m t j", t=4, j=4)[:, quads, :, :]
+                src = w1_raw[piece][:].rearrange("p j (m t) -> p m t j", t=4)[:, first:last, :, :]
+                nc.gpsimd.tensor_scalar(dst, src, 1.0, 0.0, MULT, ADD)
+                return
+            dst = w1_grouped[g][:].rearrange("p (t m j) -> p m j t", t=4, j=4)[:, quads, :, :]
             src = w1_raw[piece][:].rearrange("p j (m t) -> p m j t", t=4)[:, first:last, :, :]
-            if on_scalar:
+            if engine == "scalar":
                 nc.scalar.copy(dst, src)
             else:
                 nc.vector.tensor_copy(dst, src)
 
-        def quantize_w1(g):
-            nc.vector.quantize_mx(out=w1_codes[g][:].bitcast(FP8X4), scales=w1_scales[g][:], in_=w1_grouped[g][:])
+        free = list(range(BANKS))
+        opened = []
+        held = {}
 
+        def take_bank(key):
+            slot = free.pop(0)
+            opened.append(key)
+            held[key] = (slot, psum.tile([P, 4 * BLOCK], F32, name=f"bank{len(opened)}", tag=f"bank{slot}"))
+            return held[key][1]
+
+        def give_back(key):
+            free.append(held[key][0])
+
+        def first_pass(g, block, t):
+            rows = slice(t * P, (t + 1) * P)
+            nc.tensor.matmul_mx(
+                out=held[g, block][1][:, t * BLOCK : (t + 1) * BLOCK],
+                lhsT=w1_codes[g][:, rows].bitcast(FP8X4),
+                lhsT_scale=w1_scales[g][:, rows],
+                rhs=x_words[block].bitcast(FP8X4),
+                rhs_scale=x_scales[:, block * BLOCK : (block + 1) * BLOCK],
+                start=True,
+                stop=True,
+            )
+
+        def quantize_w1(g):
+            take_bank((g, 0))
+            take_bank((g, 1))
+            for t in range(4):
+                rows = slice(t * P, (t + 1) * P)
+                nc.vector.quantize_mx(
+                    out=w1_codes[g][:, rows].bitcast(FP8X4),
+                    scales=w1_scales[g][:, rows],
+                    in_=w1_grouped[g][:, 4 * t * P : 4 * (t + 1) * P],
+                )
+                first_pass(g, 0, t)
+                first_pass(g, 1, t)
+
+        starts = [sum(PART_BLOCKS[:part]) for part in range(PARTS)]
+        runs = (
+            [(starts[part], PART_BLOCKS[part]) for part in range(PARTS)],
+            [(starts[part], PART_BLOCKS[part]) for part in range(PARTS)],
+        )
         h_grouped = {}
         h_codes = {}
         h_scales = {}
-        for c in range(CHUNKS):
-            for g in range(GROUPS):
-                h_grouped[c, g] = keep.tile([P, 4 * CHUNK], BF16, name=f"h_grouped{c}{g}", align_bytes=256)
-                h_codes[c, g] = keep.tile([P, CHUNK], U32, name=f"h_codes{c}{g}", align_bytes=256)
-                h_scales[c, g] = keep.tile([P, CHUNK], U8, name=f"h_scales{c}{g}", align_bytes=256)
+        slots = {(0, 0): "w1_raw4"}
 
-        banks_done = []
-        banks_taken = []
+        def hidden_tile(g, block):
+            run = max(number for number, (first, count) in enumerate(runs[g]) if first <= block)
+            first, count = runs[g][run]
+            if (g, run) not in h_grouped:
+                h_grouped[g, run] = sbuf([P, 4 * count * BLOCK], BF16, f"h_grouped{g}_{run}", slots.get((g, run)))
+            return h_grouped[g, run][:, 4 * (block - first) * BLOCK : 4 * (block - first + 1) * BLOCK]
 
-        def next_bank():
-            number = len(banks_taken)
-            banks_taken.append(number)
-            return psum.tile([P, 4 * BLOCK], F32, name=f"bank{number}", tag=f"bank{number % 8}")
-
-        def hidden(c, g, block):
-            bank = next_bank()
-            cols = slice(block * BLOCK, (block + 1) * BLOCK)
-            listed = slice(c * CHUNK + block * BLOCK, c * CHUNK + (block + 1) * BLOCK)
-            for t in range(4):
-                rows = slice(t * P, (t + 1) * P)
-                nc.tensor.matmul_mx(
-                    out=bank[:, t * BLOCK : (t + 1) * BLOCK],
-                    lhsT=w1_codes[g][:, rows].bitcast(FP8X4),
-                    lhsT_scale=w1_scales[g][:, rows],
-                    rhs=x_words[c][:, cols].bitcast(FP8X4),
-                    rhs_scale=x_scales[:, listed],
-                    start=True,
-                    stop=True,
-                )
-            dst = h_grouped[c, g][:, 4 * BLOCK * block : 4 * BLOCK * (block + 1)].rearrange("p (n t) -> p n t", t=4)
-            src = bank[:].rearrange("p (t n) -> p n t", t=4)
-            number = len(banks_done)
-            banks_done.append(number)
-            if number in (1, 3, 5) or number > 8 and number % 3 == 2:
-                nc.vector.tensor_scalar_max(dst, src, 0.0)
-            else:
+        def relu(g, block, engine):
+            dst = hidden_tile(g, block).rearrange("p (n t) -> p n t", t=4)
+            src = held[g, block][1][:].rearrange("p (t n) -> p n t", t=4)
+            if engine == "scalar":
                 nc.scalar.activation(dst, src, RELU)
+            else:
+                nc.vector.tensor_scalar_max(dst, src, 0.0)
+            give_back((g, block))
 
-        def warm(c, widths):
-            bank = next_bank()
-            first = c * CHUNK
-            for width in widths:
+        def quantize_h(g, run):
+            first, count = runs[g][run]
+            codes = sbuf([P, count * BLOCK], U32, f"h_codes{g}_{run}")
+            scales = sbuf([P, count * BLOCK], U8, f"h_scales{g}_{run}")
+            nc.vector.quantize_mx(out=codes[:].bitcast(FP8X4), scales=scales[:], in_=h_grouped[g, run][:])
+            for part in range(PARTS):
+                if first <= starts[part] < first + count:
+                    cols = slice((starts[part] - first) * BLOCK, (starts[part] - first + PART_BLOCKS[part]) * BLOCK)
+                    h_codes[g, part] = codes[:, cols]
+                    h_scales[g, part] = scales[:, cols]
+
+        def second_passes(g, part):
+            last = part == PARTS - 1
+            width = PART_BLOCKS[part] * BLOCK
+            for m in range(2):
+                rows = slice(m * P, (m + 1) * P)
+                key = ("y", part, m if last else 0)
+                if key not in held:
+                    take_bank(key)
+                column = 0 if last else m * width
+                if g == 0:
+                    weights = w8[:, rows].bitcast(FP8X4)
+                else:
+                    weights = w4[:, 2 * m * P : 2 * (m + 1) * P].bitcast(FP4X4)
                 nc.tensor.matmul_mx(
-                    out=bank[:, 0:width],
-                    lhsT=x_words[c][:, 0:P].bitcast(FP8X4),
-                    lhsT_scale=picked_scales[:, first : first + P],
-                    rhs=x_words[c][:, 0:width].bitcast(FP8X4),
-                    rhs_scale=picked_scales[:, first : first + width],
-                    start=True,
-                    stop=True,
+                    out=held[key][1][:, column : column + width],
+                    lhsT=weights,
+                    lhsT_scale=w_scales[:, g, rows],
+                    rhs=h_codes[g, part].bitcast(FP8X4),
+                    rhs_scale=h_scales[g, part],
+                    start=g == 0 and (last or m == 0),
+                    stop=g == 1 and (last or m == 1),
                 )
-
-        def quantize(c, g, block0, blocks):
-            cols = slice(block0 * BLOCK, (block0 + blocks) * BLOCK)
-            nc.vector.quantize_mx(
-                out=h_codes[c, g][:, cols].bitcast(FP8X4),
-                scales=h_scales[c, g][:, cols],
-                in_=h_grouped[c, g][:, 4 * BLOCK * block0 : 4 * BLOCK * (block0 + blocks)],
-            )
 
         out_hbm = out.rearrange("(m p) j -> p m j", p=P)
 
-        def output(c, block0, blocks, width, halves):
-            total = blocks * BLOCK
-            stage = keep.tile([P, len(halves), total], F32, name=f"stage{c}_{block0}_{halves[0][0]}", align_bytes=256)
-            for i, (m, on_scalar) in enumerate(halves):
-                acc = next_bank()
-                rows = slice(m * P, (m + 1) * P)
-                passes = [(1, n, width) for n in range(0, total, width)]
-                if width == total:
-                    passes = passes + [(0, 0, total)]
+        def output(part, engines):
+            last = part == PARTS - 1
+            width = PART_BLOCKS[part] * BLOCK
+            stage = sbuf([P, 2, width], F32, f"stage{part}")
+            for m, engine in enumerate(engines):
+                key = ("y", part, m if last else 0)
+                column = 0 if last else m * width
+                src = held[key][1][:, column : column + width]
+                if engine == "scalar":
+                    nc.scalar.activation(stage[:, m, :], src, IDENTITY, bias=bias[:, m : m + 1])
                 else:
-                    passes = [(0, 0, total)] + passes
-                for number, (g, n, count) in enumerate(passes):
-                    cols = slice(block0 * BLOCK + n, block0 * BLOCK + n + count)
-                    if g == 0:
-                        weights = w8[:, rows].bitcast(FP8X4)
-                    else:
-                        weights = w4[:, 2 * m * P : 2 * (m + 1) * P].bitcast(FP4X4)
-                    nc.tensor.matmul_mx(
-                        out=acc[:, n : n + count],
-                        lhsT=weights,
-                        lhsT_scale=w_scales[:, g, rows],
-                        rhs=h_codes[c, g][:, cols].bitcast(FP8X4),
-                        rhs_scale=h_scales[c, g][:, cols],
-                        start=number == 0,
-                        stop=number == len(passes) - 1,
-                    )
-                if on_scalar:
-                    nc.scalar.activation(stage[:, i, :], acc[:, 0:total], IDENTITY, bias=bias[:, m : m + 1])
+                    nc.vector.tensor_scalar(stage[:, m, :], src, bias[:, m : m + 1], None, ADD)
+                if last or m == 1:
+                    give_back(key)
+            first = starts[part] * BLOCK
+            nc.sync.dma_start(out_hbm[:, :, first : first + width], stage[:])
+
+        fills = [
+            ("w1", 0), ("h", 0, 2), ("h", 0, 3), ("h", 0, 4), ("h", 0, 5), ("h", 0, 6),
+            ("h", 0, 7), ("h", 0, 8), ("h", 0, 9), ("h", 0, 10), ("h", 0, 11), ("w1", 1),
+            ("h", 1, 2), ("h", 1, 3), ("h", 1, 4), ("h", 1, 5), ("h", 1, 6), ("h", 1, 7),
+            ("y", 0, 0), ("y", 1, 0), ("h", 1, 8), ("h", 1, 9), ("y", 0, 1), ("y", 1, 1),
+            ("h", 1, 10), ("h", 1, 11), ("y", 0, 2), ("y", 1, 2), ("y", 0, 3), ("y", 1, 3),
+            ("y", 0, 4), ("y", 1, 4), ("y", 0, 5), ("y", 1, 5),
+        ]
+
+        def fill():
+            while fills:
+                kind = fills[0][0]
+                if kind == "w1":
+                    return
+                kind, g, number = fills[0]
+                if kind == "h":
+                    if not free or number not in x_words:
+                        return
+                    take_bank((g, number))
+                    for t in range(4):
+                        first_pass(g, number, t)
                 else:
-                    nc.vector.tensor_scalar(stage[:, i, :], acc[:, 0:total], bias[:, m : m + 1], None, ADD)
-            first = c * CHUNK + block0 * BLOCK
-            m0 = halves[0][0]
-            nc.sync.dma_start(out_hbm[:, m0 : m0 + len(halves), first : first + total], stage[:])
+                    needed = 0 if g == 1 else 2 if number == PARTS - 1 else 1
+                    if len(free) < needed or (g, number) not in h_codes:
+                        return
+                    second_passes(g, number)
+                fills.pop(0)
 
-        gather_words(0, "x_words0")
-        warm(0, [CHUNK, CHUNK, CHUNK, CHUNK // 2])
-        gather_words(1, "x_words1")
-        for piece in range(3):
-            convert(piece, 0, WIDTHS[piece] // 4, True)
-        convert(3, 0, SCALAR_SHARE, True)
-        convert(3, SCALAR_SHARE, WIDTHS[3] // 4, False)
-        quantize_w1(0)
-        gather_words(2, "w1_grouped0")
-        convert(4, 0, WIDTHS[4] // 4, True)
-        order = w1_grouped[1][:].rearrange("p (t m j) -> p m t j", t=4, j=4)
-        nc.gpsimd.tensor_scalar(
-            order[:, WIDTHS[4] // 4 : GROUP // 4, :, :], w1_raw[5][:].rearrange("p j (m t) -> p m t j", t=4), 1.0, 0.0, MULT, ADD
-        )
+        def start_group(g):
+            assert fills[0] == ("w1", g)
+            fills.pop(0)
+            quantize_w1(g)
 
-        runs = [(0, 0, 0, 4), (1, 0, 0, 4), (2, 0, 0, 2), (0, 1, 0, 4), (1, 1, 0, 4), (2, 1, 0, 2), (2, 0, 2, 2), (2, 1, 2, 2)]
-        steps = [(c, g, block) for c, g, block0, blocks in runs for block in range(block0, block0 + blocks)]
-        due = {}
-        end = 0
-        for run in runs:
-            end = end + run[3]
-            due[end - 1 + LAG] = run
-        for number, (c, g, block) in enumerate(steps):
-            if number == BLOCKS:
-                quantize_w1(1)
-            hidden(c, g, block)
-            if number in due:
-                quantize(*due[number])
-            if number == len(steps) - 3:
-                output(0, 0, 4, 512, [(0, False)])
-            if number == len(steps) - 2:
-                output(0, 0, 4, 512, [(1, True)])
-        for number in sorted(due):
-            if number >= len(steps):
-                quantize(*due[number])
-        output(1, 0, 4, 512, [(0, True)])
-        output(1, 0, 4, 512, [(1, True)])
-        output(2, 0, 2, 128, [(0, True), (1, False)])
-        output(2, 2, 2, 128, [(0, True), (1, False)])
+        scalar, vector, gpsimd = "scalar", "vector", "gpsimd"
+        first_words = gather(0)
+        warm = take_bank("warm")
+        for width in WARM_WIDTHS:
+            nc.tensor.matmul_mx(
+                out=warm[:, 0:width],
+                lhsT=first_words[:, 0:P].bitcast(FP8X4),
+                lhsT_scale=picked_scales[:, 0:P],
+                rhs=first_words[:, 0:width].bitcast(FP8X4),
+                rhs_scale=picked_scales[:, 0:width],
+                start=True,
+                stop=True,
+            )
+        give_back("warm")
+        gather(1)
+        convert(0, 0, 32, scalar)
+        convert(1, 0, 32, scalar)
+        convert(2, 0, 32, scalar)
+        convert(3, 0, 32 - VECTOR_SHARE, scalar)
+        gather(2)
+        convert(3, 32 - VECTOR_SHARE, 32, vector)
+        start_group(0)
+        convert(4, 0, 32, scalar)
+        convert(5, 0, 24, scalar)
+        gather(3, "w1_raw3")
+        convert(6, 0, 72, gpsimd)
+
+        steps = [
+            (relu, 0, 0, scalar), (relu, 0, 1, vector), (relu, 0, 2, scalar), (relu, 0, 3, vector),
+            (relu, 0, 4, scalar), (relu, 0, 5, vector), (relu, 0, 6, scalar), (relu, 0, 7, vector),
+            (relu, 0, 8, scalar), (start_group, 1), (relu, 0, 9, scalar), (relu, 0, 10, vector),
+            (relu, 0, 11, scalar), (relu, 1, 0, vector), (relu, 1, 1, scalar), (quantize_h, 0, 0),
+            (quantize_h, 1, 0), (relu, 1, 2, scalar), (quantize_h, 0, 1), (relu, 1, 3, scalar),
+            (relu, 1, 4, vector), (relu, 1, 5, scalar), (quantize_h, 0, 2), (quantize_h, 1, 1),
+            (quantize_h, 1, 2), (output, 0, (scalar, scalar)), (relu, 1, 6, vector), (relu, 1, 7, scalar),
+            (quantize_h, 0, 3), (quantize_h, 1, 3), (output, 1, (scalar, scalar)), (relu, 1, 8, vector),
+            (relu, 1, 9, scalar), (quantize_h, 0, 4), (quantize_h, 1, 4), (output, 2, (scalar, scalar)),
+            (relu, 1, 10, vector), (relu, 1, 11, scalar), (quantize_h, 0, 5), (quantize_h, 1, 5),
+            (output, 3, (scalar, scalar)), (output, 4, (scalar, scalar)), (output, 5, (vector, scalar)),
+        ]
+        for step in steps:
+            fill()
+            step[0](*step[1:])

@@ -25,15 +25,16 @@ BLOCK = 128
 CHUNK = 512
 GROUP = 512
 BLOCKS = S // BLOCK
-PART_BLOCKS = (2, 2, 2, 2, 2, 2)
+PART_BLOCKS = (4, 4, 2, 2)
+RUN_BLOCKS = (4, 4, 2, 2)
 PARTS = len(PART_BLOCKS)
-WIDTHS = (128, 128, 128, 128, 128, 96, 288)
-GATHERS = (512, 512, 256, 256)
+BANK_EACH = (0, 1, 2, 3)
+WIDTHS = (128, 128, 128, 128, 128, 128, 256)
+GATHERS = (512, 512, 512)
 FIRST_COLUMNS = 768
 VECTOR_SHARE = 12
 PLACES = dict(
-    [("h_grouped0_4", 0), ("w_rows", 1792), ("w1_scales1", 2048), ("h_grouped0_5", 2560), ("w1_grouped1", 4608)]
-    + [(f"h_scales0_{part}", 4608 + 256 * part) for part in range(6)]
+    [("w_rows", 0), ("w1_scales1", 0)] + [(f"h_scales0_{run}", 512 + 512 * run) for run in range(len(RUN_BLOCKS))]
 )
 WARM_WIDTHS = (512, 512, 512, 256)
 
@@ -60,7 +61,7 @@ def tile_list_tabmlp_mix_bias_kernel(
         nc.vector.memset(table_scales[:].bitcast(I32), 0)
         nc.sync.dma_start(table_words[:, 0:FIRST_COLUMNS], words_hbm[:, 0:FIRST_COLUMNS])
         nc.sync.dma_start(offsets[:], offs)
-        w_rows = sbuf([P, 2, 2 * M], U8, "w_rows")
+        w_rows = sbuf([P, 2, 7 * M], U8, "w_rows")
         for g, src in enumerate((w8_scales, w4_scales)):
             nc.sync.dma_start(w_rows[32:96:4, g, 0:M].bitcast(I32), src[0].bitcast(I32))
         nc.sync.dma_start(table_scales[32:96:4, :].bitcast(I32), scales_hbm)
@@ -85,15 +86,15 @@ def tile_list_tabmlp_mix_bias_kernel(
         for piece in range(5, len(WIDTHS)):
             load_w1(piece)
 
-        w8 = sbuf([P, M], I32, "w8")
-        nc.sync.dma_start(w8[:], w8_words[0].rearrange("p n i -> p (n i)").bitcast(I32))
-        w4 = sbuf([P, 2 * M], U8, "w4")
-        nc.sync.dma_start(w4[:].bitcast(I32), w4_words[0].bitcast(I32))
         w_scales = sbuf([P, 2, M], U8, "w_scales")
         nc.vector.memset(w_scales[:].rearrange("p g n -> p (g n)").bitcast(I32), 0)
         for r in range(4):
             rows = w_rows[32 + 4 * r : 96 : 16, :, 0:M]
             nc.sync.dma_start(w_scales[r:P:32, :, :].bitcast(I32), rows.bitcast(I32))
+        w8 = sbuf([P, M], I32, "w8")
+        nc.sync.dma_start(w8[:], w8_words[0].rearrange("p n i -> p (n i)").bitcast(I32))
+        w4 = sbuf([P, 2 * M], U8, "w4")
+        nc.sync.dma_start(w4[:].bitcast(I32), w4_words[0].bitcast(I32))
         bias = sbuf([P, 2], F32, "bias")
         nc.sync.dma_start(bias[:], b.rearrange("(m p) -> p m", p=P))
 
@@ -168,7 +169,7 @@ def tile_list_tabmlp_mix_bias_kernel(
 
         starts = [sum(PART_BLOCKS[:part]) for part in range(PARTS)]
         runs = (
-            [(starts[part], PART_BLOCKS[part]) for part in range(PARTS)],
+            [(sum(RUN_BLOCKS[:run]), RUN_BLOCKS[run]) for run in range(len(RUN_BLOCKS))],
             [(starts[part], PART_BLOCKS[part]) for part in range(PARTS)],
         )
         h_grouped = {}
@@ -203,55 +204,58 @@ def tile_list_tabmlp_mix_bias_kernel(
                     h_codes[g, part] = codes[:, cols]
                     h_scales[g, part] = scales[:, cols]
 
-        def second_passes(g, part):
-            last = part == PARTS - 1
+        def place(part, m):
             width = PART_BLOCKS[part] * BLOCK
-            for m in range(2):
+            if part in BANK_EACH:
+                return ("y", part, m), slice(0, width)
+            return ("y", part, 0), slice(m * width, (m + 1) * width)
+
+        def second_passes(g, part, halves):
+            for m in halves:
                 rows = slice(m * P, (m + 1) * P)
-                key = ("y", part, m if last else 0)
+                key, cols = place(part, m)
                 if key not in held:
                     take_bank(key)
-                column = 0 if last else m * width
                 if g == 0:
                     weights = w8[:, rows].bitcast(FP8X4)
                 else:
                     weights = w4[:, 2 * m * P : 2 * (m + 1) * P].bitcast(FP4X4)
                 nc.tensor.matmul_mx(
-                    out=held[key][1][:, column : column + width],
+                    out=held[key][1][:, cols],
                     lhsT=weights,
                     lhsT_scale=w_scales[:, g, rows],
                     rhs=h_codes[g, part].bitcast(FP8X4),
                     rhs_scale=h_scales[g, part],
-                    start=g == 0 and (last or m == 0),
-                    stop=g == 1 and (last or m == 1),
+                    start=g == 0 and (part in BANK_EACH or m == 0),
+                    stop=g == 1 and (part in BANK_EACH or m == 1),
                 )
 
         out_hbm = out.rearrange("(m p) j -> p m j", p=P)
 
-        def output(part, engines):
-            last = part == PARTS - 1
+        def output(part, halves):
             width = PART_BLOCKS[part] * BLOCK
-            stage = sbuf([P, 2, width], F32, f"stage{part}")
-            for m, engine in enumerate(engines):
-                key = ("y", part, m if last else 0)
-                column = 0 if last else m * width
-                src = held[key][1][:, column : column + width]
+            m0 = halves[0][0]
+            stage = sbuf([P, len(halves), width], F32, f"stage{part}_{m0}")
+            for m, engine in halves:
+                key, cols = place(part, m)
+                src = held[key][1][:, cols]
                 if engine == "scalar":
-                    nc.scalar.activation(stage[:, m, :], src, IDENTITY, bias=bias[:, m : m + 1])
+                    nc.scalar.activation(stage[:, m - m0, :], src, IDENTITY, bias=bias[:, m : m + 1])
                 else:
-                    nc.vector.tensor_scalar(stage[:, m, :], src, bias[:, m : m + 1], None, ADD)
-                if last or m == 1:
+                    nc.vector.tensor_scalar(stage[:, m - m0, :], src, bias[:, m : m + 1], None, ADD)
+                if part in BANK_EACH or m == 1:
                     give_back(key)
             first = starts[part] * BLOCK
-            nc.sync.dma_start(out_hbm[:, :, first : first + width], stage[:])
+            nc.sync.dma_start(out_hbm[:, m0 : m0 + len(halves), first : first + width], stage[:])
 
         fills = [
-            ("w1", 0), ("h", 0, 2), ("h", 0, 3), ("h", 0, 4), ("h", 0, 5), ("h", 0, 6),
-            ("h", 0, 7), ("h", 0, 8), ("h", 0, 9), ("h", 0, 10), ("h", 0, 11), ("w1", 1),
-            ("h", 1, 2), ("h", 1, 3), ("h", 1, 4), ("h", 1, 5), ("h", 1, 6), ("h", 1, 7),
-            ("y", 0, 0), ("y", 1, 0), ("h", 1, 8), ("h", 1, 9), ("y", 0, 1), ("y", 1, 1),
-            ("h", 1, 10), ("h", 1, 11), ("y", 0, 2), ("y", 1, 2), ("y", 0, 3), ("y", 1, 3),
-            ("y", 0, 4), ("y", 1, 4), ("y", 0, 5), ("y", 1, 5),
+            ("w1", 0), ("h", 0, 2), ("h", 0, 3), ("h", 0, 4), ("h", 0, 5),
+            ("h", 0, 6), ("h", 0, 7), ("h", 0, 8), ("h", 0, 9), ("w1", 1),
+            ("h", 1, 2), ("h", 1, 3), ("h", 1, 4), ("h", 1, 5), ("h", 1, 6),
+            ("h", 1, 7), ("h", 1, 8), ("h", 1, 9), ("h", 0, 10), ("h", 0, 11),
+            ("y", 0, 0, (0,)), ("y", 1, 0, (0,)), ("y", 0, 0, (1,)), ("y", 1, 0, (1,)), ("h", 1, 10),
+            ("h", 1, 11), ("y", 0, 1, (0,)), ("y", 1, 1, (0,)), ("y", 0, 1, (1,)), ("y", 1, 1, (1,)),
+            ("y", 0, 2, (0, 1)), ("y", 1, 2, (0, 1)), ("y", 0, 3, (0, 1)), ("y", 1, 3, (0, 1)),
         ]
 
         def fill():
@@ -259,7 +263,7 @@ def tile_list_tabmlp_mix_bias_kernel(
                 kind = fills[0][0]
                 if kind == "w1":
                     return
-                kind, g, number = fills[0]
+                kind, g, number = fills[0][0:3]
                 if kind == "h":
                     if not free or number not in x_words:
                         return
@@ -267,10 +271,11 @@ def tile_list_tabmlp_mix_bias_kernel(
                     for t in range(4):
                         first_pass(g, number, t)
                 else:
-                    needed = 0 if g == 1 else 2 if number == PARTS - 1 else 1
+                    halves = fills[0][3]
+                    needed = len(set(place(number, m)[0] for m in halves if place(number, m)[0] not in held))
                     if len(free) < needed or (g, number) not in h_codes:
                         return
-                    second_passes(g, number)
+                    second_passes(g, number, halves)
                 fills.pop(0)
 
         def start_group(g):
@@ -297,26 +302,27 @@ def tile_list_tabmlp_mix_bias_kernel(
         convert(1, 0, 32, scalar)
         convert(2, 0, 32, scalar)
         convert(3, 0, 32 - VECTOR_SHARE, scalar)
-        gather(2)
         convert(3, 32 - VECTOR_SHARE, 32, vector)
         start_group(0)
         convert(4, 0, 32, scalar)
-        convert(5, 0, 24, scalar)
-        gather(3, "w1_raw3")
-        convert(6, 0, 72, gpsimd)
+        convert(5, 0, 32, scalar)
+        gather(2, "w1_raw3")
+        convert(6, 0, 64, gpsimd)
 
         steps = [
-            (relu, 0, 0, scalar), (relu, 0, 1, vector), (relu, 0, 2, scalar), (relu, 0, 3, vector),
-            (relu, 0, 4, scalar), (relu, 0, 5, vector), (relu, 0, 6, scalar), (relu, 0, 7, vector),
-            (relu, 0, 8, scalar), (start_group, 1), (relu, 0, 9, scalar), (relu, 0, 10, vector),
-            (relu, 0, 11, scalar), (relu, 1, 0, vector), (relu, 1, 1, scalar), (quantize_h, 0, 0),
-            (quantize_h, 1, 0), (relu, 1, 2, scalar), (quantize_h, 0, 1), (relu, 1, 3, scalar),
-            (relu, 1, 4, vector), (relu, 1, 5, scalar), (quantize_h, 0, 2), (quantize_h, 1, 1),
-            (quantize_h, 1, 2), (output, 0, (scalar, scalar)), (relu, 1, 6, vector), (relu, 1, 7, scalar),
-            (quantize_h, 0, 3), (quantize_h, 1, 3), (output, 1, (scalar, scalar)), (relu, 1, 8, vector),
-            (relu, 1, 9, scalar), (quantize_h, 0, 4), (quantize_h, 1, 4), (output, 2, (scalar, scalar)),
-            (relu, 1, 10, vector), (relu, 1, 11, scalar), (quantize_h, 0, 5), (quantize_h, 1, 5),
-            (output, 3, (scalar, scalar)), (output, 4, (scalar, scalar)), (output, 5, (vector, scalar)),
+            (relu, 0, 0, scalar), (relu, 0, 1, vector), (relu, 0, 2, scalar),
+            (relu, 0, 3, vector), (relu, 0, 4, scalar), (relu, 0, 5, vector),
+            (relu, 0, 6, scalar), (start_group, 1), (relu, 0, 7, scalar),
+            (quantize_h, 0, 0), (relu, 0, 8, scalar), (relu, 0, 9, scalar),
+            (relu, 1, 0, scalar), (quantize_h, 0, 1), (relu, 1, 1, vector),
+            (relu, 1, 2, scalar), (quantize_h, 0, 2), (relu, 1, 3, scalar),
+            (relu, 1, 4, vector), (relu, 1, 5, scalar), (relu, 1, 6, scalar),
+            (quantize_h, 1, 0), (relu, 1, 7, vector), (relu, 1, 8, scalar),
+            (relu, 0, 10, vector), (relu, 1, 9, scalar), (quantize_h, 1, 1),
+            (relu, 0, 11, vector), (output, 0, ((0, scalar),)), (output, 0, ((1, scalar),)),
+            (quantize_h, 1, 2), (relu, 1, 10, scalar), (relu, 1, 11, vector),
+            (quantize_h, 0, 3), (quantize_h, 1, 3), (output, 1, ((0, scalar),)),
+            (output, 1, ((1, scalar),)), (output, 2, ((0, scalar), (1, vector))), (output, 3, ((0, scalar), (1, vector))),
         ]
         for step in steps:
             fill()

@@ -24,19 +24,13 @@ BANKS = 8
 BLOCK = 128
 CHUNK = 512
 GROUP = 512
-BLOCKS = S // BLOCK
-PART_BLOCKS = (4, 4, 2, 2)
-RUN_BLOCKS = (4, 4, 2, 2)
-PARTS = len(PART_BLOCKS)
-BANK_EACH = (0, 1, 2, 3)
+PARTS = ((0, 4), (4, 4), (8, 2), (10, 2))
 WIDTHS = (128, 128, 128, 128, 128, 128, 256)
-GATHERS = (512, 512, 512)
 FIRST_COLUMNS = 768
 VECTOR_SHARE = 12
-PLACES = dict(
-    [("w_rows", 0), ("w1_scales1", 0)] + [(f"h_scales0_{run}", 512 + 512 * run) for run in range(len(RUN_BLOCKS))]
-)
+LAG = 3
 WARM_WIDTHS = (512, 512, 512, 256)
+ROWS_PITCH = 7 * M
 
 
 def tile_list_tabmlp_mix_bias_kernel(
@@ -49,9 +43,17 @@ def tile_list_tabmlp_mix_bias_kernel(
         psum = ctx.enter_context(tc.psum_pool(name="psum", bufs=1))
 
         def sbuf(shape, dtype, name, slot=None):
-            if name in PLACES:
-                return shared.tile(shape, dtype, name=name, offset=PLACES[name], align_bytes=ALIGN)
             return keep.tile(shape, dtype, name=name, tag=slot or name, align_bytes=ALIGN)
+
+        def on_scale_rows(shape, name, offset):
+            return shared.tile(shape, U8, name=name, offset=offset, align_bytes=ALIGN)
+
+        opened = []
+
+        def next_bank():
+            bank = psum.tile([P, 4 * BLOCK], F32, name=f"bank{len(opened)}", tag=f"bank{len(opened) % BANKS}")
+            opened.append(bank)
+            return bank
 
         offsets = sbuf([P, S // 16], U16, "offsets")
         table_words = sbuf([P, T], I32, "table_words")
@@ -61,7 +63,7 @@ def tile_list_tabmlp_mix_bias_kernel(
         nc.vector.memset(table_scales[:].bitcast(I32), 0)
         nc.sync.dma_start(table_words[:, 0:FIRST_COLUMNS], words_hbm[:, 0:FIRST_COLUMNS])
         nc.sync.dma_start(offsets[:], offs)
-        w_rows = sbuf([P, 2, 7 * M], U8, "w_rows")
+        w_rows = on_scale_rows([P, 2, ROWS_PITCH], "w_rows", 0)
         for g, src in enumerate((w8_scales, w4_scales)):
             nc.sync.dma_start(w_rows[32:96:4, g, 0:M].bitcast(I32), src[0].bitcast(I32))
         nc.sync.dma_start(table_scales[32:96:4, :].bitcast(I32), scales_hbm)
@@ -100,19 +102,14 @@ def tile_list_tabmlp_mix_bias_kernel(
 
         x_words = {}
 
-        def gather(number, slot=None):
-            first = sum(GATHERS[:number])
-            count = GATHERS[number]
-            words = sbuf([P, count], U32, f"x_words{number}", slot)
-            listed = offsets[:, first // 16 : (first + count) // 16]
-            nc.vector.tensor_copy(words[:], table_words[:].bitcast(U32).indirect(listed))
-            for start in range(0, count, BLOCK):
-                x_words[(first + start) // BLOCK] = words[:, start : start + BLOCK]
-            return words
+        def gather(chunk, slot=None):
+            x_words[chunk] = sbuf([P, CHUNK], U32, f"x_words{chunk}", slot)
+            listed = offsets[:, chunk * CHUNK // 16 : (chunk + 1) * CHUNK // 16]
+            nc.vector.tensor_copy(x_words[chunk][:], table_words[:].bitcast(U32).indirect(listed))
 
         w1_grouped = [sbuf([P, 4 * GROUP], BF16, f"w1_grouped{g}") for g in range(2)]
         w1_codes = [sbuf([P, GROUP], U32, f"w1_codes{g}") for g in range(2)]
-        w1_scales = [sbuf([P, GROUP], U8, f"w1_scales{g}") for g in range(2)]
+        w1_scales = [sbuf([P, GROUP], U8, "w1_scales0"), on_scale_rows([P, GROUP], "w1_scales1", 0)]
 
         def convert(piece, first, last, engine):
             g, start = divmod(sum(WIDTHS[:piece]), GROUP)
@@ -129,34 +126,7 @@ def tile_list_tabmlp_mix_bias_kernel(
             else:
                 nc.vector.tensor_copy(dst, src)
 
-        free = list(range(BANKS))
-        opened = []
-        held = {}
-
-        def take_bank(key):
-            slot = free.pop(0)
-            opened.append(key)
-            held[key] = (slot, psum.tile([P, 4 * BLOCK], F32, name=f"bank{len(opened)}", tag=f"bank{slot}"))
-            return held[key][1]
-
-        def give_back(key):
-            free.append(held[key][0])
-
-        def first_pass(g, block, t):
-            rows = slice(t * P, (t + 1) * P)
-            nc.tensor.matmul_mx(
-                out=held[g, block][1][:, t * BLOCK : (t + 1) * BLOCK],
-                lhsT=w1_codes[g][:, rows].bitcast(FP8X4),
-                lhsT_scale=w1_scales[g][:, rows],
-                rhs=x_words[block].bitcast(FP8X4),
-                rhs_scale=x_scales[:, block * BLOCK : (block + 1) * BLOCK],
-                start=True,
-                stop=True,
-            )
-
         def quantize_w1(g):
-            take_bank((g, 0))
-            take_bank((g, 1))
             for t in range(4):
                 rows = slice(t * P, (t + 1) * P)
                 nc.vector.quantize_mx(
@@ -164,166 +134,130 @@ def tile_list_tabmlp_mix_bias_kernel(
                     scales=w1_scales[g][:, rows],
                     in_=w1_grouped[g][:, 4 * t * P : 4 * (t + 1) * P],
                 )
-                first_pass(g, 0, t)
-                first_pass(g, 1, t)
 
-        starts = [sum(PART_BLOCKS[:part]) for part in range(PARTS)]
-        runs = (
-            [(sum(RUN_BLOCKS[:run]), RUN_BLOCKS[run]) for run in range(len(RUN_BLOCKS))],
-            [(starts[part], PART_BLOCKS[part]) for part in range(PARTS)],
-        )
+        filled = {}
+
+        def fill(g, blocks):
+            for block in blocks:
+                filled[g, block] = next_bank()
+            for t in range(4):
+                rows = slice(t * P, (t + 1) * P)
+                for block in blocks:
+                    chunk, start = divmod(block * BLOCK, CHUNK)
+                    nc.tensor.matmul_mx(
+                        out=filled[g, block][:, t * BLOCK : (t + 1) * BLOCK],
+                        lhsT=w1_codes[g][:, rows].bitcast(FP8X4),
+                        lhsT_scale=w1_scales[g][:, rows],
+                        rhs=x_words[chunk][:, start : start + BLOCK].bitcast(FP8X4),
+                        rhs_scale=x_scales[:, block * BLOCK : (block + 1) * BLOCK],
+                        start=True,
+                        stop=True,
+                    )
+
         h_grouped = {}
         h_codes = {}
         h_scales = {}
-        slots = {(0, 0): "w1_raw4"}
 
-        def hidden_tile(g, block):
-            run = max(number for number, (first, count) in enumerate(runs[g]) if first <= block)
-            first, count = runs[g][run]
-            if (g, run) not in h_grouped:
-                h_grouped[g, run] = sbuf([P, 4 * count * BLOCK], BF16, f"h_grouped{g}_{run}", slots.get((g, run)))
-            return h_grouped[g, run][:, 4 * (block - first) * BLOCK : 4 * (block - first + 1) * BLOCK]
-
-        def relu(g, block, engine):
-            dst = hidden_tile(g, block).rearrange("p (n t) -> p n t", t=4)
-            src = held[g, block][1][:].rearrange("p (t n) -> p n t", t=4)
-            if engine == "scalar":
-                nc.scalar.activation(dst, src, RELU)
-            else:
+        def relu(g, part, block, on_vector):
+            first, count = PARTS[part]
+            if (g, part) not in h_grouped:
+                slot = "w1_raw4" if (g, part) == (0, 0) else None
+                h_grouped[g, part] = sbuf([P, 4 * count * BLOCK], BF16, f"h_grouped{g}_{part}", slot)
+            window = h_grouped[g, part][:, 4 * (block - first) * BLOCK : 4 * (block - first + 1) * BLOCK]
+            dst = window.rearrange("p (n t) -> p n t", t=4)
+            src = filled[g, block][:].rearrange("p (t n) -> p n t", t=4)
+            if on_vector:
                 nc.vector.tensor_scalar_max(dst, src, 0.0)
-            give_back((g, block))
+            else:
+                nc.scalar.activation(dst, src, RELU)
 
-        def quantize_h(g, run):
-            first, count = runs[g][run]
-            codes = sbuf([P, count * BLOCK], U32, f"h_codes{g}_{run}")
-            scales = sbuf([P, count * BLOCK], U8, f"h_scales{g}_{run}")
-            nc.vector.quantize_mx(out=codes[:].bitcast(FP8X4), scales=scales[:], in_=h_grouped[g, run][:])
-            for part in range(PARTS):
-                if first <= starts[part] < first + count:
-                    cols = slice((starts[part] - first) * BLOCK, (starts[part] - first + PART_BLOCKS[part]) * BLOCK)
-                    h_codes[g, part] = codes[:, cols]
-                    h_scales[g, part] = scales[:, cols]
-
-        def place(part, m):
-            width = PART_BLOCKS[part] * BLOCK
-            if part in BANK_EACH:
-                return ("y", part, m), slice(0, width)
-            return ("y", part, 0), slice(m * width, (m + 1) * width)
-
-        def second_passes(g, part, halves):
-            for m in halves:
-                rows = slice(m * P, (m + 1) * P)
-                key, cols = place(part, m)
-                if key not in held:
-                    take_bank(key)
-                if g == 0:
-                    weights = w8[:, rows].bitcast(FP8X4)
-                else:
-                    weights = w4[:, 2 * m * P : 2 * (m + 1) * P].bitcast(FP4X4)
-                nc.tensor.matmul_mx(
-                    out=held[key][1][:, cols],
-                    lhsT=weights,
-                    lhsT_scale=w_scales[:, g, rows],
-                    rhs=h_codes[g, part].bitcast(FP8X4),
-                    rhs_scale=h_scales[g, part],
-                    start=g == 0 and (part in BANK_EACH or m == 0),
-                    stop=g == 1 and (part in BANK_EACH or m == 1),
-                )
+        def quantize_h(g, part):
+            width = PARTS[part][1] * BLOCK
+            h_codes[g, part] = sbuf([P, width], U32, f"h_codes{g}_{part}")
+            if g == 0:
+                h_scales[g, part] = on_scale_rows([P, width], f"h_scales0_{part}", CHUNK * (part + 1))
+            else:
+                h_scales[g, part] = sbuf([P, width], U8, f"h_scales1_{part}")
+            nc.vector.quantize_mx(
+                out=h_codes[g, part][:].bitcast(FP8X4), scales=h_scales[g, part][:], in_=h_grouped[g, part][:]
+            )
 
         out_hbm = out.rearrange("(m p) j -> p m j", p=P)
 
         def output(part, halves):
-            width = PART_BLOCKS[part] * BLOCK
+            first, count = PARTS[part]
+            width = count * BLOCK
+            sums = [next_bank() for half in halves]
+            for g in range(2):
+                for acc, (m, on_vector) in zip(sums, halves):
+                    if g == 0:
+                        weights = w8[:, m * P : (m + 1) * P].bitcast(FP8X4)
+                    else:
+                        weights = w4[:, 2 * m * P : 2 * (m + 1) * P].bitcast(FP4X4)
+                    nc.tensor.matmul_mx(
+                        out=acc[:, 0:width],
+                        lhsT=weights,
+                        lhsT_scale=w_scales[:, g, m * P : (m + 1) * P],
+                        rhs=h_codes[g, part][:].bitcast(FP8X4),
+                        rhs_scale=h_scales[g, part][:],
+                        start=g == 0,
+                        stop=g == 1,
+                    )
             m0 = halves[0][0]
             stage = sbuf([P, len(halves), width], F32, f"stage{part}_{m0}")
-            for m, engine in halves:
-                key, cols = place(part, m)
-                src = held[key][1][:, cols]
-                if engine == "scalar":
-                    nc.scalar.activation(stage[:, m - m0, :], src, IDENTITY, bias=bias[:, m : m + 1])
+            for acc, (m, on_vector) in zip(sums, halves):
+                if on_vector:
+                    nc.vector.tensor_scalar(stage[:, m - m0, :], acc[:, 0:width], bias[:, m : m + 1], None, ADD)
                 else:
-                    nc.vector.tensor_scalar(stage[:, m - m0, :], src, bias[:, m : m + 1], None, ADD)
-                if part in BANK_EACH or m == 1:
-                    give_back(key)
-            first = starts[part] * BLOCK
-            nc.sync.dma_start(out_hbm[:, m0 : m0 + len(halves), first : first + width], stage[:])
+                    nc.scalar.activation(stage[:, m - m0, :], acc[:, 0:width], IDENTITY, bias=bias[:, m : m + 1])
+            cols = slice(first * BLOCK, first * BLOCK + width)
+            nc.sync.dma_start(out_hbm[:, m0 : m0 + len(halves), cols], stage[:])
 
-        fills = [
-            ("w1", 0), ("h", 0, 2), ("h", 0, 3), ("h", 0, 4), ("h", 0, 5),
-            ("h", 0, 6), ("h", 0, 7), ("h", 0, 8), ("h", 0, 9), ("w1", 1),
-            ("h", 1, 2), ("h", 1, 3), ("h", 1, 4), ("h", 1, 5), ("h", 1, 6),
-            ("h", 1, 7), ("h", 1, 8), ("h", 1, 9), ("h", 0, 10), ("h", 0, 11),
-            ("y", 0, 0, (0,)), ("y", 1, 0, (0,)), ("y", 0, 0, (1,)), ("y", 1, 0, (1,)), ("h", 1, 10),
-            ("h", 1, 11), ("y", 0, 1, (0,)), ("y", 1, 1, (0,)), ("y", 0, 1, (1,)), ("y", 1, 1, (1,)),
-            ("y", 0, 2, (0, 1)), ("y", 1, 2, (0, 1)), ("y", 0, 3, (0, 1)), ("y", 1, 3, (0, 1)),
-        ]
-
-        def fill():
-            while fills:
-                kind = fills[0][0]
-                if kind == "w1":
-                    return
-                kind, g, number = fills[0][0:3]
-                if kind == "h":
-                    if not free or number not in x_words:
-                        return
-                    take_bank((g, number))
-                    for t in range(4):
-                        first_pass(g, number, t)
-                else:
-                    halves = fills[0][3]
-                    needed = len(set(place(number, m)[0] for m in halves if place(number, m)[0] not in held))
-                    if len(free) < needed or (g, number) not in h_codes:
-                        return
-                    second_passes(g, number, halves)
-                fills.pop(0)
-
-        def start_group(g):
-            assert fills[0] == ("w1", g)
-            fills.pop(0)
-            quantize_w1(g)
-
-        scalar, vector, gpsimd = "scalar", "vector", "gpsimd"
-        first_words = gather(0)
-        warm = take_bank("warm")
+        gather(0)
+        warm = next_bank()
         for width in WARM_WIDTHS:
             nc.tensor.matmul_mx(
                 out=warm[:, 0:width],
-                lhsT=first_words[:, 0:P].bitcast(FP8X4),
+                lhsT=x_words[0][:, 0:P].bitcast(FP8X4),
                 lhsT_scale=picked_scales[:, 0:P],
-                rhs=first_words[:, 0:width].bitcast(FP8X4),
+                rhs=x_words[0][:, 0:width].bitcast(FP8X4),
                 rhs_scale=picked_scales[:, 0:width],
                 start=True,
                 stop=True,
             )
-        give_back("warm")
         gather(1)
-        convert(0, 0, 32, scalar)
-        convert(1, 0, 32, scalar)
-        convert(2, 0, 32, scalar)
-        convert(3, 0, 32 - VECTOR_SHARE, scalar)
-        convert(3, 32 - VECTOR_SHARE, 32, vector)
-        start_group(0)
-        convert(4, 0, 32, scalar)
-        convert(5, 0, 32, scalar)
+        for piece in range(3):
+            convert(piece, 0, 32, "scalar")
+        convert(3, 0, 32 - VECTOR_SHARE, "scalar")
+        convert(3, 32 - VECTOR_SHARE, 32, "vector")
+        quantize_w1(0)
+        convert(4, 0, 32, "scalar")
+        convert(5, 0, 32, "scalar")
         gather(2, "w1_raw3")
-        convert(6, 0, 64, gpsimd)
+        convert(6, 0, 64, "gpsimd")
 
-        steps = [
-            (relu, 0, 0, scalar), (relu, 0, 1, vector), (relu, 0, 2, scalar),
-            (relu, 0, 3, vector), (relu, 0, 4, scalar), (relu, 0, 5, vector),
-            (relu, 0, 6, scalar), (start_group, 1), (relu, 0, 7, scalar),
-            (quantize_h, 0, 0), (relu, 0, 8, scalar), (relu, 0, 9, scalar),
-            (relu, 1, 0, scalar), (quantize_h, 0, 1), (relu, 1, 1, vector),
-            (relu, 1, 2, scalar), (quantize_h, 0, 2), (relu, 1, 3, scalar),
-            (relu, 1, 4, vector), (relu, 1, 5, scalar), (relu, 1, 6, scalar),
-            (quantize_h, 1, 0), (relu, 1, 7, vector), (relu, 1, 8, scalar),
-            (relu, 0, 10, vector), (relu, 1, 9, scalar), (quantize_h, 1, 1),
-            (relu, 0, 11, vector), (output, 0, ((0, scalar),)), (output, 0, ((1, scalar),)),
-            (quantize_h, 1, 2), (relu, 1, 10, scalar), (relu, 1, 11, vector),
-            (quantize_h, 0, 3), (quantize_h, 1, 3), (output, 1, ((0, scalar),)),
-            (output, 1, ((1, scalar),)), (output, 2, ((0, scalar), (1, vector))), (output, 3, ((0, scalar), (1, vector))),
-        ]
-        for step in steps:
-            fill()
-            step[0](*step[1:])
+        last = len(PARTS) - 1
+        runs = [(g, part) for g in range(2) for part in range(last)] + [(g, last) for g in range(2)]
+        banks = [(g, part, PARTS[part][0] + i) for g, part in runs for i in range(PARTS[part][1])]
+        pending = []
+        for number, (g, part, block) in enumerate(banks):
+            if block == 0:
+                fill(g, (0, 1))
+            elif block > 1:
+                fill(g, (block,))
+            relu(g, part, block, number in (1, 3, 5) or (number > 8 and number % 3 == 2) or (g, part) == (0, last))
+            if number == 6:
+                quantize_w1(1)
+            if block == sum(PARTS[part]) - 1:
+                pending.append((number + LAG, g, part))
+            while pending and pending[0][0] <= number:
+                quantize_h(*pending.pop(0)[1:])
+            if (g, block) == (0, sum(PARTS[last]) - 1):
+                output(0, [(0, False)])
+                output(0, [(1, False)])
+        for due, g, part in pending:
+            quantize_h(g, part)
+        output(1, [(0, False)])
+        output(1, [(1, False)])
+        output(2, [(0, False), (1, True)])
+        output(3, [(0, False), (1, True)])

@@ -126,13 +126,13 @@ def tile_list_tabmlp_mix_bias_kernel(
             else:
                 nc.vector.tensor_copy(dst, src)
 
-        def quantize_w1(g):
+        def quantize_w1(g, first=0, last=P):
             for t in range(4):
-                rows = slice(t * P, (t + 1) * P)
+                rows = slice(t * P + first, t * P + last)
                 nc.vector.quantize_mx(
                     out=w1_codes[g][:, rows].bitcast(FP8X4),
                     scales=w1_scales[g][:, rows],
-                    in_=w1_grouped[g][:, 4 * t * P : 4 * (t + 1) * P],
+                    in_=w1_grouped[g][:, 4 * rows.start : 4 * rows.stop],
                 )
 
         filled = {}
@@ -226,11 +226,13 @@ def tile_list_tabmlp_mix_bias_kernel(
                 stop=True,
             )
         gather(1)
-        for piece in range(3):
-            convert(piece, 0, 32, "scalar")
+        convert(0, 0, 32, "scalar")
+        convert(1, 0, 32, "scalar")
+        quantize_w1(0, 0, P // 2)
+        convert(2, 0, 32, "scalar")
         convert(3, 0, 32 - VECTOR_SHARE, "scalar")
         convert(3, 32 - VECTOR_SHARE, 32, "vector")
-        quantize_w1(0)
+        quantize_w1(0, P // 2, P)
         convert(4, 0, 32, "scalar")
         convert(5, 0, 32, "scalar")
         gather(2, "w1_raw3")

@@ -29,7 +29,8 @@ WIDTHS = (128, 128, 128, 128, 128, 128, 256)
 FIRST_COLUMNS = 768
 VECTOR_SHARE = 12
 LAG = 3
-WARM_WIDTHS = (512, 512, 512, 256)
+WARM_PASSES = 6
+WARM_ROWS = 64
 ROWS_PITCH = 7 * M
 
 
@@ -213,18 +214,19 @@ def tile_list_tabmlp_mix_bias_kernel(
             cols = slice(first * BLOCK, first * BLOCK + width)
             nc.sync.dma_start(out_hbm[:, m0 : m0 + len(halves), cols], stage[:])
 
-        gather(0)
         warm = next_bank()
-        for width in WARM_WIDTHS:
+        warm_words = table_words[:, T - CHUNK : T]
+        for repeat in range(WARM_PASSES):
             nc.tensor.matmul_mx(
-                out=warm[:, 0:width],
-                lhsT=x_words[0][:, 0:P].bitcast(FP8X4),
-                lhsT_scale=picked_scales[:, 0:P],
-                rhs=x_words[0][:, 0:width].bitcast(FP8X4),
-                rhs_scale=picked_scales[:, 0:width],
+                out=warm[0:WARM_ROWS, :],
+                lhsT=warm_words[:, 0:WARM_ROWS].bitcast(FP8X4),
+                lhsT_scale=picked_scales[:, 0:WARM_ROWS],
+                rhs=warm_words.bitcast(FP8X4),
+                rhs_scale=picked_scales[:, 0:CHUNK],
                 start=True,
                 stop=True,
             )
+        gather(0)
         gather(1)
         convert(0, 0, 32, "scalar")
         convert(1, 0, 32, "scalar")

@@ -238,7 +238,7 @@ def tile_list_tabmlp_mix_bias_kernel(
         convert(4, 0, 32, "scalar")
         convert(5, 0, 32, "scalar")
         gather(2, "w1_raw3")
-        convert(6, 0, 64, "gpsimd")
+        convert(6, 0, 64, "vector")
 
         last = len(PARTS) - 1
         runs = [(g, part) for g in range(2) for part in range(last)] + [(g, last) for g in range(2)]

@@ -24,8 +24,9 @@ BANKS = 8
 BLOCK = 128
 CHUNK = 512
 GROUP = 512
+PIECE = 128
+QUADS = PIECE // 4
 PARTS = ((0, 4), (4, 4), (8, 2), (10, 2))
-WIDTHS = (128, 128, 128, 128, 128, 128, 256)
 FIRST_COLUMNS = 768
 VECTOR_SHARE = 12
 LAG = 3
@@ -74,9 +75,8 @@ def tile_list_tabmlp_mix_bias_kernel(
         w1_raw = {}
 
         def load_w1(piece):
-            start = sum(WIDTHS[:piece])
-            w1_raw[piece] = sbuf([P, 4, WIDTHS[piece]], F32, f"w1_raw{piece}")
-            nc.sync.dma_start(w1_raw[piece][:], w1_hbm[:, :, start : start + WIDTHS[piece]])
+            w1_raw[piece] = sbuf([P, 4, PIECE], F32, f"w1_raw{piece}")
+            nc.sync.dma_start(w1_raw[piece][:], w1_hbm[:, :, piece * PIECE : (piece + 1) * PIECE])
 
         for piece in range(5):
             load_w1(piece)
@@ -86,16 +86,17 @@ def tile_list_tabmlp_mix_bias_kernel(
         nc.vector.tensor_copy(picked_scales[:], table_scales[:].indirect(offsets[:]))
         for r in range(4):
             nc.sync.dma_start(x_scales[r:P:32, :].bitcast(I32), picked_scales[32 + 4 * r : 96 : 16, :].bitcast(I32))
-        for piece in range(5, len(WIDTHS)):
+        for piece in (6, 7):
             load_w1(piece)
+        w8 = sbuf([P, M], I32, "w8")
+        nc.sync.dma_start(w8[:], w8_words[0].rearrange("p n i -> p (n i)").bitcast(I32))
+        load_w1(5)
 
         w_scales = sbuf([P, 2, M], U8, "w_scales")
         nc.vector.memset(w_scales[:].rearrange("p g n -> p (g n)").bitcast(I32), 0)
         for r in range(4):
             rows = w_rows[32 + 4 * r : 96 : 16, :, 0:M]
             nc.sync.dma_start(w_scales[r:P:32, :, :].bitcast(I32), rows.bitcast(I32))
-        w8 = sbuf([P, M], I32, "w8")
-        nc.sync.dma_start(w8[:], w8_words[0].rearrange("p n i -> p (n i)").bitcast(I32))
         w4 = sbuf([P, 2 * M], U8, "w4")
         nc.sync.dma_start(w4[:].bitcast(I32), w4_words[0].bitcast(I32))
         bias = sbuf([P, 2], F32, "bias")
@@ -108,32 +109,35 @@ def tile_list_tabmlp_mix_bias_kernel(
             listed = offsets[:, chunk * CHUNK // 16 : (chunk + 1) * CHUNK // 16]
             nc.vector.tensor_copy(x_words[chunk][:], table_words[:].bitcast(U32).indirect(listed))
 
-        w1_grouped = [sbuf([P, 4 * GROUP], BF16, f"w1_grouped{g}") for g in range(2)]
+        w1_half = {}
         w1_codes = [sbuf([P, GROUP], U32, f"w1_codes{g}") for g in range(2)]
         w1_scales = [sbuf([P, GROUP], U8, "w1_scales0"), on_scale_rows([P, GROUP], "w1_scales1", 0)]
 
         def convert(piece, first, last, engine):
-            g, start = divmod(sum(WIDTHS[:piece]), GROUP)
-            quads = slice(start // 4 + first, start // 4 + last)
+            half = piece // 2
+            if half not in w1_half:
+                w1_half[half] = sbuf([P, 8 * PIECE], BF16, f"w1_half{half}", "w1_half1" if half == 3 else None)
+            quads = slice(piece % 2 * QUADS + first, piece % 2 * QUADS + last)
             if engine == "gpsimd":
-                dst = w1_grouped[g][:].rearrange("p (t m j) -> p m t j", t=4, j=4)[:, quads, :, :]
+                dst = w1_half[half][:].rearrange("p (t m j) -> p m t j", t=4, j=4)[:, quads, :, :]
                 src = w1_raw[piece][:].rearrange("p j (m t) -> p m t j", t=4)[:, first:last, :, :]
                 nc.gpsimd.tensor_scalar(dst, src, 1.0, 0.0, MULT, ADD)
                 return
-            dst = w1_grouped[g][:].rearrange("p (t m j) -> p m j t", t=4, j=4)[:, quads, :, :]
+            dst = w1_half[half][:].rearrange("p (t m j) -> p m j t", t=4, j=4)[:, quads, :, :]
             src = w1_raw[piece][:].rearrange("p j (m t) -> p m j t", t=4)[:, first:last, :, :]
             if engine == "scalar":
                 nc.scalar.copy(dst, src)
             else:
                 nc.vector.tensor_copy(dst, src)
 
-        def quantize_w1(g, first=0, last=P):
+        def quantize_w1(half):
+            g, upper = divmod(half, 2)
             for t in range(4):
-                rows = slice(t * P + first, t * P + last)
+                rows = slice(t * P + upper * P // 2, t * P + (upper + 1) * P // 2)
                 nc.vector.quantize_mx(
                     out=w1_codes[g][:, rows].bitcast(FP8X4),
                     scales=w1_scales[g][:, rows],
-                    in_=w1_grouped[g][:, 4 * rows.start : 4 * rows.stop],
+                    in_=w1_half[half][:, t * 2 * PIECE : (t + 1) * 2 * PIECE],
                 )
 
         filled = {}
@@ -228,30 +232,32 @@ def tile_list_tabmlp_mix_bias_kernel(
             )
         gather(0)
         gather(1)
-        convert(0, 0, 32, "scalar")
-        convert(1, 0, 32, "scalar")
-        quantize_w1(0, 0, P // 2)
-        convert(2, 0, 32, "scalar")
-        convert(3, 0, 32 - VECTOR_SHARE, "scalar")
-        convert(3, 32 - VECTOR_SHARE, 32, "vector")
-        quantize_w1(0, P // 2, P)
-        convert(4, 0, 32, "scalar")
-        convert(5, 0, 32, "scalar")
+        convert(0, 0, QUADS, "scalar")
+        convert(1, 0, QUADS, "scalar")
+        quantize_w1(0)
+        convert(2, 0, QUADS, "scalar")
+        convert(3, 0, QUADS - VECTOR_SHARE, "scalar")
+        convert(3, QUADS - VECTOR_SHARE, QUADS, "vector")
+        quantize_w1(1)
+        convert(4, 0, QUADS, "scalar")
         gather(2, "w1_raw3")
-        convert(6, 0, 64, "vector")
+        convert(6, 0, QUADS, "gpsimd")
+        convert(7, 0, QUADS, "gpsimd")
 
         last = len(PARTS) - 1
         runs = [(g, part) for g in range(2) for part in range(last)] + [(g, last) for g in range(2)]
         banks = [(g, part, PARTS[part][0] + i) for g, part in runs for i in range(PARTS[part][1])]
         pending = []
         for number, (g, part, block) in enumerate(banks):
-            if block == 0:
+            if (g, block) == (1, 0):
                 fill(g, (0, 1))
-            elif block > 1:
+            elif (g, block) != (1, 1):
                 fill(g, (block,))
             relu(g, part, block, number in (1, 3, 5) or (number > 8 and number % 3 == 2) or (g, part) == (0, last))
-            if number == 6:
-                quantize_w1(1)
+            if number == 5:
+                convert(5, 0, QUADS, "vector")
+                quantize_w1(3)
+                quantize_w1(2)
             if block == sum(PARTS[part]) - 1:
                 pending.append((number + LAG, g, part))
             while pending and pending[0][0] <= number:

@@ -28,9 +28,9 @@ PIECE = 128
 QUADS = PIECE // 4
 PARTS = ((0, 4), (4, 4), (8, 2), (10, 2))
 FIRST_COLUMNS = 768
-VECTOR_SHARE = 12
+VECTOR_SHARE = 16
 LAG = 3
-WARM_PASSES = 6
+WARM_PASSES = 5
 WARM_ROWS = 64
 ROWS_PITCH = 7 * M
 
@@ -234,10 +234,10 @@ def tile_list_tabmlp_mix_bias_kernel(
         gather(1)
         convert(0, 0, QUADS, "scalar")
         convert(1, 0, QUADS, "scalar")
-        quantize_w1(0)
         convert(2, 0, QUADS, "scalar")
         convert(3, 0, QUADS - VECTOR_SHARE, "scalar")
         convert(3, QUADS - VECTOR_SHARE, QUADS, "vector")
+        quantize_w1(0)
         quantize_w1(1)
         convert(4, 0, QUADS, "scalar")
         gather(2, "w1_raw3")

from contextlib import ExitStack

import concourse.mybir as mybir

K, H, M, T, S = 512, 1024, 256, 4096, 1536
FLOPS = 2 * S * (K * H + H * M)

F32 = mybir.dt.float32
BF16 = mybir.dt.bfloat16
I32 = mybir.dt.int32
U32 = mybir.dt.uint32
U16 = mybir.dt.uint16
U8 = mybir.dt.uint8
FP8X4 = mybir.dt.float8_e4m3fn_x4
FP4X4 = mybir.dt.float4_e2m1fn_x4
RELU = mybir.ActivationFunctionType.Relu
IDENTITY = mybir.ActivationFunctionType.Identity
ADD = mybir.AluOpType.add
MULT = mybir.AluOpType.mult

P = 128
ALIGN = 256
BANKS = 8
BLOCK = 128
CHUNK = 512
GROUP = 512
PIECE = 128
QUADS = PIECE // 4
PARTS = ((0, 4), (4, 4), (8, 2), (10, 2))
FIRST_COLUMNS = 768
VECTOR_SHARE = 16
LAG = 3
WARM_PASSES = 5
WARM_ROWS = 64
ROWS_PITCH = 7 * M


def tile_list_tabmlp_mix_bias_kernel(
    tc, tab, w1, w8_words, w8_scales, w4_words, w4_scales, b, offs, out
):
    nc = tc.nc
    with ExitStack() as ctx:
        keep = ctx.enter_context(tc.tile_pool(name="keep", bufs=1))
        shared = ctx.enter_context(tc.tile_pool(name="shared", bufs=1))
        psum = ctx.enter_context(tc.psum_pool(name="psum", bufs=1))

        def sbuf(shape, dtype, name, slot=None):
            return keep.tile(shape, dtype, name=name, tag=slot or name, align_bytes=ALIGN)

        def on_scale_rows(shape, name, offset):
            return shared.tile(shape, U8, name=name, offset=offset, align_bytes=ALIGN)

        opened = []

        def next_bank():
            bank = psum.tile([P, 4 * BLOCK], F32, name=f"bank{len(opened)}", tag=f"bank{len(opened) % BANKS}")
            opened.append(bank)
            return bank

        offsets = sbuf([P, S // 16], U16, "offsets")
        table_words = sbuf([P, T], I32, "table_words")
        table_scales = sbuf([P, T], U8, "table_scales")
        words_hbm = tab[0, 0 : 512 * T].rearrange("(p c) -> p c", p=P).bitcast(I32)
        scales_hbm = tab[0, 512 * T : 528 * T].rearrange("(q t) -> q t", q=16).bitcast(I32)
        nc.vector.memset(table_scales[:].bitcast(I32), 0)
        nc.sync.dma_start(table_words[:, 0:FIRST_COLUMNS], words_hbm[:, 0:FIRST_COLUMNS])
        nc.sync.dma_start(offsets[:], offs)
        w_rows = on_scale_rows([P, 2, ROWS_PITCH], "w_rows", 0)
        for g, src in enumerate((w8_scales, w4_scales)):
            nc.sync.dma_start(w_rows[32:96:4, g, 0:M].bitcast(I32), src[0].bitcast(I32))
        nc.sync.dma_start(table_scales[32:96:4, :].bitcast(I32), scales_hbm)
        nc.sync.dma_start(table_words[:, FIRST_COLUMNS:T], words_hbm[:, FIRST_COLUMNS:T])

        w1_hbm = w1.rearrange("(p j) c -> p j c", j=4)
        w1_raw = {}

        def load_w1(piece):
            w1_raw[piece] = sbuf([P, 4, PIECE], F32, f"w1_raw{piece}")
            nc.sync.dma_start(w1_raw[piece][:], w1_hbm[:, :, piece * PIECE : (piece + 1) * PIECE])

        for piece in range(5):
            load_w1(piece)
        x_scales = sbuf([P, S], U8, "x_scales")
        nc.vector.memset(x_scales[:].bitcast(I32), 0)
        picked_scales = sbuf([P, S], U8, "picked_scales")
        nc.vector.tensor_copy(picked_scales[:], table_scales[:].indirect(offsets[:]))
        for r in range(4):
            nc.sync.dma_start(x_scales[r:P:32, :].bitcast(I32), picked_scales[32 + 4 * r : 96 : 16, :].bitcast(I32))
        for piece in (6, 7):
            load_w1(piece)
        w8 = sbuf([P, M], I32, "w8")
        nc.sync.dma_start(w8[:], w8_words[0].rearrange("p n i -> p (n i)").bitcast(I32))
        load_w1(5)

        w_scales = sbuf([P, 2, M], U8, "w_scales")
        nc.vector.memset(w_scales[:].rearrange("p g n -> p (g n)").bitcast(I32), 0)
        for r in range(4):
            rows = w_rows[32 + 4 * r : 96 : 16, :, 0:M]
            nc.sync.dma_start(w_scales[r:P:32, :, :].bitcast(I32), rows.bitcast(I32))
        w4 = sbuf([P, 2 * M], U8, "w4")
        nc.sync.dma_start(w4[:].bitcast(I32), w4_words[0].bitcast(I32))
        bias = sbuf([P, 2], F32, "bias")
        nc.sync.dma_start(bias[:], b.rearrange("(m p) -> p m", p=P))

        x_words = {}

        def gather(chunk, slot=None):
            x_words[chunk] = sbuf([P, CHUNK], U32, f"x_words{chunk}", slot)
            listed = offsets[:, chunk * CHUNK // 16 : (chunk + 1) * CHUNK // 16]
            nc.vector.tensor_copy(x_words[chunk][:], table_words[:].bitcast(U32).indirect(listed))

        w1_half = {}
        w1_codes = [sbuf([P, GROUP], U32, f"w1_codes{g}") for g in range(2)]
        w1_scales = [sbuf([P, GROUP], U8, "w1_scales0"), on_scale_rows([P, GROUP], "w1_scales1", 0)]

        def convert(piece, first, last, engine):
            half = piece // 2
            if half not in w1_half:
                w1_half[half] = sbuf([P, 8 * PIECE], BF16, f"w1_half{half}", "w1_half1" if half == 3 else None)
            quads = slice(piece % 2 * QUADS + first, piece % 2 * QUADS + last)
            if engine == "gpsimd":
                dst = w1_half[half][:].rearrange("p (t m j) -> p m t j", t=4, j=4)[:, quads, :, :]
                src = w1_raw[piece][:].rearrange("p j (m t) -> p m t j", t=4)[:, first:last, :, :]
                nc.gpsimd.tensor_scalar(dst, src, 1.0, 0.0, MULT, ADD)
                return
            dst = w1_half[half][:].rearrange("p (t m j) -> p m j t", t=4, j=4)[:, quads, :, :]
            src = w1_raw[piece][:].rearrange("p j (m t) -> p m j t", t=4)[:, first:last, :, :]
            if engine == "scalar":
                nc.scalar.copy(dst, src)
            else:
                nc.vector.tensor_copy(dst, src)

        def quantize_w1(half):
            g, upper = divmod(half, 2)
            for t in range(4):
                rows = slice(t * P + upper * P // 2, t * P + (upper + 1) * P // 2)
                nc.vector.quantize_mx(
                    out=w1_codes[g][:, rows].bitcast(FP8X4),
                    scales=w1_scales[g][:, rows],
                    in_=w1_half[half][:, t * 2 * PIECE : (t + 1) * 2 * PIECE],
                )

        filled = {}

        def fill(g, blocks):
            for block in blocks:
                filled[g, block] = next_bank()
            for t in range(4):
                rows = slice(t * P, (t + 1) * P)
                for block in blocks:
                    chunk, start = divmod(block * BLOCK, CHUNK)
                    nc.tensor.matmul_mx(
                        out=filled[g, block][:, t * BLOCK : (t + 1) * BLOCK],
                        lhsT=w1_codes[g][:, rows].bitcast(FP8X4),
                        lhsT_scale=w1_scales[g][:, rows],
                        rhs=x_words[chunk][:, start : start + BLOCK].bitcast(FP8X4),
                        rhs_scale=x_scales[:, block * BLOCK : (block + 1) * BLOCK],
                        start=True,
                        stop=True,
                    )

        h_grouped = {}
        h_codes = {}
        h_scales = {}

        def relu(g, part, block, on_vector):
            first, count = PARTS[part]
            if (g, part) not in h_grouped:
                slot = "w1_raw4" if (g, part) == (0, 0) else None
                h_grouped[g, part] = sbuf([P, 4 * count * BLOCK], BF16, f"h_grouped{g}_{part}", slot)
            window = h_grouped[g, part][:, 4 * (block - first) * BLOCK : 4 * (block - first + 1) * BLOCK]
            dst = window.rearrange("p (n t) -> p n t", t=4)
            src = filled[g, block][:].rearrange("p (t n) -> p n t", t=4)
            if on_vector:
                nc.vector.tensor_scalar_max(dst, src, 0.0)
            else:
                nc.scalar.activation(dst, src, RELU)

        def quantize_h(g, part):
            width = PARTS[part][1] * BLOCK
            h_codes[g, part] = sbuf([P, width], U32, f"h_codes{g}_{part}")
            if g == 0:
                h_scales[g, part] = on_scale_rows([P, width], f"h_scales0_{part}", CHUNK * (part + 1))
            else:
                h_scales[g, part] = sbuf([P, width], U8, f"h_scales1_{part}")
            nc.vector.quantize_mx(
                out=h_codes[g, part][:].bitcast(FP8X4), scales=h_scales[g, part][:], in_=h_grouped[g, part][:]
            )

        out_hbm = out.rearrange("(m p) j -> p m j", p=P)

        def output(part, halves):
            first, count = PARTS[part]
            width = count * BLOCK
            sums = [next_bank() for half in halves]
            for g in range(2):
                for acc, (m, on_vector) in zip(sums, halves):
                    if g == 0:
                        weights = w8[:, m * P : (m + 1) * P].bitcast(FP8X4)
                    else:
                        weights = w4[:, 2 * m * P : 2 * (m + 1) * P].bitcast(FP4X4)
                    nc.tensor.matmul_mx(
                        out=acc[:, 0:width],
                        lhsT=weights,
                        lhsT_scale=w_scales[:, g, m * P : (m + 1) * P],
                        rhs=h_codes[g, part][:].bitcast(FP8X4),
                        rhs_scale=h_scales[g, part][:],
                        start=g == 0,
                        stop=g == 1,
                    )
            m0 = halves[0][0]
            stage = sbuf([P, len(halves), width], F32, f"stage{part}_{m0}")
            for acc, (m, on_vector) in zip(sums, halves):
                if on_vector:
                    nc.vector.tensor_scalar(stage[:, m - m0, :], acc[:, 0:width], bias[:, m : m + 1], None, ADD)
                else:
                    nc.scalar.activation(stage[:, m - m0, :], acc[:, 0:width], IDENTITY, bias=bias[:, m : m + 1])
            cols = slice(first * BLOCK, first * BLOCK + width)
            nc.sync.dma_start(out_hbm[:, m0 : m0 + len(halves), cols], stage[:])

        warm = next_bank()
        warm_words = table_words[:, T - CHUNK : T]
        for repeat in range(WARM_PASSES):
            nc.tensor.matmul_mx(
                out=warm[0:WARM_ROWS, :],
                lhsT=warm_words[:, 0:WARM_ROWS].bitcast(FP8X4),
                lhsT_scale=picked_scales[:, 0:WARM_ROWS],
                rhs=warm_words.bitcast(FP8X4),
                rhs_scale=picked_scales[:, 0:CHUNK],
                start=True,
                stop=True,
            )
        gather(0)
        gather(1)
        convert(0, 0, QUADS, "scalar")
        convert(1, 0, QUADS, "scalar")
        convert(2, 0, QUADS, "scalar")
        convert(3, 0, QUADS - VECTOR_SHARE, "scalar")
        convert(3, QUADS - VECTOR_SHARE, QUADS, "vector")
        quantize_w1(0)
        quantize_w1(1)
        convert(4, 0, QUADS, "scalar")
        gather(2, "w1_raw3")
        convert(6, 0, QUADS, "gpsimd")
        convert(7, 0, QUADS, "gpsimd")

        last = len(PARTS) - 1
        runs = [(g, part) for g in range(2) for part in range(last)] + [(g, last) for g in range(2)]
        banks = [(g, part, PARTS[part][0] + i) for g, part in runs for i in range(PARTS[part][1])]
        pending = []
        for number, (g, part, block) in enumerate(banks):
            if (g, block) == (1, 0):
                fill(g, (0, 1))
            elif (g, block) != (1, 1):
                fill(g, (block,))
            relu(g, part, block, number in (1, 3, 5) or (number > 8 and number % 3 == 2) or (g, part) == (0, last))
            if number == 5:
                convert(5, 0, QUADS, "vector")
                quantize_w1(3)
                quantize_w1(2)
            if block == sum(PARTS[part]) - 1:
                pending.append((number + LAG, g, part))
            while pending and pending[0][0] <= number:
                quantize_h(*pending.pop(0)[1:])
            if (g, block) == (0, sum(PARTS[last]) - 1):
                output(0, [(0, False)])
                output(0, [(1, False)])
        for due, g, part in pending:
            quantize_h(g, part)
        output(1, [(0, False)])
        output(1, [(1, False)])
        output(2, [(0, False), (1, True)])
        output(3, [(0, False), (1, True)])
